import numpy as np, ml_dtypes
CORES = [14,30,46,142,158,174,270,286,302,398,414,430]
N = 12
R, L = 4096, 1024
CAPP = 256
def entries(a): return a.T.reshape(-1)
def pack(v, P): return np.ascontiguousarray(np.asarray(v, np.int32).reshape(-1, P).T)
def lists(rng, how):
    n = N * L
    P = rng.permutation(np.repeat(np.arange(N * N), CAPP))[:n]
    if how == "full":
        a, b = rng.permutation(N)[:2]; o = rng.permutation(N * N); o = o[(o // N != a) & (o % N != b)]
        C = np.concatenate([N * a + rng.permutation(np.delete(np.arange(N), b)), [N * a + b], N * rng.permutation(np.delete(np.arange(N), a)) + b, o])[:n // CAPP]
        P = np.repeat(C, CAPP).reshape(N, L)[rng.permutation(N)].reshape(-1)
    h, g = P // N, P % N
    d = np.zeros(n, np.int64)
    for q in range(N): m = np.nonzero(g == q)[0]; d[m] = R * q + np.concatenate([[0, R - 1], 1 + rng.permutation(R - 2)])[:len(m)]
    s = R * h + rng.integers(0, R, n)
    if how == "fork": s = R * h + rng.integers(0, R, N)[h]
    if how == "chain":
        for q in range(N):
            m = np.nonzero(h == q)[0]; w = d[g == q]
            if len(w): s[m] = w[rng.integers(0, len(w), len(m))]
    if how == "gaps":
        z = rng.permutation(N)[:3]; k = (rng.random(n) < 0.5) | (np.arange(n) // L == z[0]) | (h == z[1]) | (g == z[2]); s[k] = -1; d[k] = -1
    return {"src": np.stack([pack(v, 16) for v in s.reshape(N, L)]), "dst": np.stack([pack(v, 16) for v in d.reshape(N, L)])}
def setup_inputs(rng):
    return dict({"tab": rng.standard_normal((N, 128, R), dtype=np.float32).astype(ml_dtypes.bfloat16)}, **lists(rng, "uniform"))
def setup_inputs_chain(rng):
    d = setup_inputs(rng); d.update(lists(rng, "chain"))
    for k in ("tab",): d[k] = (d[k].astype(np.float32) * 1048576.0).astype(d[k].dtype)
    return d
def setup_inputs_fork(rng):
    d = setup_inputs(rng); d.update(lists(rng, "fork"))
    for k in ("tab",): d[k] = (d[k].astype(np.float32) * (1 / 1024.0)).astype(d[k].dtype)
    return d
def setup_inputs_full(rng):
    d = setup_inputs(rng); d.update(lists(rng, "full"))
    return d
def setup_inputs_gaps(rng):
    d = setup_inputs(rng); d.update(lists(rng, "gaps"))
    return d
def check_inputs(x):
    bad = []; s, d = x["src"].reshape(-1), x["dst"].reshape(-1); k = d >= 0
    if s.min() < -1 or s.max() >= N * R or d.min() < -1 or d.max() >= N * R: bad.append("out of range")
    if ((s < 0) != (d < 0)).any(): bad.append("half a pair")
    if len(np.unique(d[k])) != int(k.sum()): bad.append("a column is written twice")
    if k.any() and int(np.bincount(s[k] // R * N + d[k] // R).max()) > CAPP: bad.append("more than CAPP pairs from one rank's part to one rank's part")
    return bad
def reference(tab, src, dst):
    A = np.concatenate(list(tab), axis=1); Y = A.copy()
    for r in range(N):
        s, d = entries(src[r]), entries(dst[r]); k = d >= 0
        Y[:, d[k]] = A[:, s[k]]
    return {"y": np.stack([Y[:, R * r:R * r + R] for r in range(N)])}

@@ -1,0 +1,535 @@
+from concourse.bass import DstId, RemoteDMATransfer
+from concourse.mybir import AluOpType, ActivationFunctionType
+
+N = 12
+CAPP = 256
+R = 4096
+L = 1024
+F = N * L // 128
+LAND = N * CAPP
+TR = 16 * F
+COPY = ActivationFunctionType.Copy
+IDENT = ActivationFunctionType.Identity
+A = AluOpType
+
+SCRATCH = {
+    "Ls": ("dram", [N, 128, L // 128], "int32"),
+    "Ld": ("dram", [N, 128, L // 128], "int32"),
+    "S": ("sbuf", [128, F], "int32"),
+    "D": ("sbuf", [128, F], "int32"),
+    "HS": ("sbuf", [128, F], "int32"),
+    "GD": ("sbuf", [128, F], "int32"),
+    "CODE": ("sbuf", [128, F], "bfloat16"),
+    "M": ("sbuf", [128, (N + 1) * F], "bfloat16"),
+    "SC": ("sbuf", [128, N * F], "bfloat16"),
+    "P": ("sbuf", [128, (N + 1) * F], "bfloat16"),
+    "BS": ("sbuf", [128, 16], "float32"),
+    "SL": ("sbuf", [128, F], "float32"),
+    "HI": ("sbuf", [128, F], "bfloat16"),
+    "LO": ("sbuf", [128, F], "bfloat16"),
+    "V": ("sbuf", [128, TR], "bfloat16"),
+    "O": ("sbuf", [128, F], "uint16"),
+    "WIN": ("sbuf", [128, R + TR], "bfloat16"),
+    "GO": ("sbuf", [128, LAND // 16], "uint16"),
+    "INV": ("sbuf", [128, R // 16], "uint16"),
+    "G": ("sbuf", [128, LAND], "bfloat16"),
+    "DG": ("sbuf", [128, 3 * CAPP], "bfloat16"),
+    "W": ("sbuf", [128, LAND + R], "bfloat16"),
+    "Y": ("sbuf", [128, R], "bfloat16"),
+    "ONE": ("sbuf", [128, 128], "bfloat16"),
+    "IDN": ("sbuf", [128, 128], "bfloat16"),
+    "TRI": ("sbuf", [128, 128], "bfloat16"),
+    "SI": ("sbuf", [128, (N + 1) * 128], "bfloat16"),
+    "SEL": ("sbuf", [128, 16 * 128], "bfloat16"),
+    "PRM": ("sbuf", [128, 4 * 128], "bfloat16"),
+    "RS": ("sbuf", [128, N * F], "bfloat16"),
+    "PI": ("sbuf", [128, 1], "int32"),
+    "QI": ("sbuf", [128, 2], "int32"),
+    "QF": ("sbuf", [128, 4], "float32"),
+    "K16": ("sbuf", [128, R // 16], "float32"),
+    "ROW8": ("sbuf", [128, 8], "float32"),
+    "C8": ("sbuf", [128, 8], "float32"),
+    "TD": ("sbuf", [128, 2 * F], "float32"),
+    "TC": ("sbuf", [128, R // 16], "float32"),
+    "MM": ("sbuf", [128, F], "float32"),
+    "U": ("sbuf", [128, 3 * F], "float32"),
+    "EE": ("sbuf", [128, 3 * R // 16], "float32"),
+}
+for _k in range(8):
+    SCRATCH["ps%d" % _k] = ("psum", [128, 512], "float32")
+SEMAPHORES = ["lp", "la", "di0", "di1", "di2", "da", "iv", "ls"] + ["e%d" % _k for _k in range(110)]
+
+
+def bits(mask):
+    return [b for b in range(mask.bit_length()) if (mask >> b) & 1]
+
+
+def together(bs):
+    return sum(1 << b for b in bs)
+
+
+def shared_engines(topo, core, dests):
+    m = topo.mask(core, dests[0])
+    for d in dests[1:]:
+        m = m & topo.mask(core, d)
+    return bits(m)
+
+
+def helper_of(c, topo):
+    near = [x for x in range(max(0, c - 7), c + 8)
+            if x != c and topo.host(x) == topo.host(c) and topo.chip(x) == topo.chip(c) and topo.die(x) == topo.die(c)]
+    return near[-1]
+
+
+def layout(T, topo, r):
+    c = T.cores[r]
+    others = [t for t in range(N) if t != r]
+    direct = [t for t in others if topo.may_write(c, T.cores[t])]
+    diag = [t for t in others if t not in direct]
+    far = [t for t in direct if topo.rack(topo.host(T.cores[t])) != topo.rack(topo.host(c))]
+    peer = [t for t in far if topo.chip(T.cores[t]) == topo.chip(c)][0]
+    near = [t for t in direct if t not in far]
+    turn = r % 3
+    diag = diag[turn:] + diag[:turn]
+    far = far[turn:] + far[:turn]
+    mate = [t for t in near if topo.host(T.cores[t]) != topo.host(c)]
+    same = [t for t in near if t not in mate]
+    near = mate[turn:] + mate[:turn] + same
+    return peer, diag, far, near, direct
+
+
+def tools(g, T):
+    st = {"n": 0}
+    q = {"g": g, "v": g.vector, "s": g.scalar, "t": g.tensor, "y": g.sync}
+    allev = []
+
+    def new():
+        k = st["n"]
+        st["n"] = k + 1
+        e = {"sem": T.sem["e%d" % k], "t": 0, "w": []}
+        allev.append(e)
+        return e
+
+    def done(inst, e, n=1):
+        inst.then_inc(e["sem"], n)
+        e["t"] = e["t"] + n
+
+    def need(name, *evs):
+        for e in evs:
+            if name not in e["w"]:
+                q[name].wait_ge(e["sem"], e["t"])
+                e["w"].append(name)
+
+    def finish():
+        for e in allev:
+            if e["t"] and not e["w"]:
+                need("g", e)
+
+    return new, done, need, finish
+
+
+def constants(g, T, tk, source):
+    new, done, need, finish = tk
+    v = g.vector
+    one, z, cg = new(), new(), new()
+    done(v.memset(T.ONE[:], 1.0), one)
+    done(v.memset(T.SEL[:], 0.0), z)
+    done(v.memset(T.PRM[:], 0.0), z)
+    done(v.memset(T.RS[:], 1.0), z)
+    done(g.iota(T.PI[:], [[1, 1]], 0, 1), cg)
+    done(g.iota(T.K16[:], [[16, R // 16]], 0, 0, allow_small_or_imprecise_dtypes=True), cg)
+    done(g.iota(T.ROW8[:], [[1, 8]], 0, 0, allow_small_or_imprecise_dtypes=True), cg)
+    need("g", one)
+    done(g.affine_select(T.IDN[:], T.ONE[:], [[-1, 128]], A.is_equal, 0.0, 0, 1), cg)
+    done(g.affine_select(T.TRI[:], T.ONE[:], [[1, 128]], A.is_gt, 0.0, 0, -1), cg)
+    cv = new()
+    need("v", z)
+    for k in range(16):
+        done(v.memset(T.SEL[:, 128 * k + k:128 * k + 128:16], 1.0), cv)
+    done(v.memset(T.RS[:, 0:N * F:F], 0.0), cv)
+    need("v", cg)
+    e1, e2, e3 = new(), new(), new()
+    done(v.tensor_scalar(T.QI[:, 0:1], T.PI[:], 15, None, A.bitwise_and), e1)
+    done(v.tensor_copy(T.PRM[:, 0:128:2], T.IDN[:, 0:128:2]), cv)
+    done(v.tensor_copy(T.PRM[:, 129:256:2], T.IDN[:, 0:128:2]), cv)
+    done(v.tensor_copy(T.PRM[:, 257:384:2], T.IDN[:, 1:128:2]), cv)
+    done(v.tensor_copy(T.PRM[:, 384:512:2], T.IDN[:, 1:128:2]), cv)
+    need("v", e1)
+    done(v.tensor_scalar(T.QI[:, 1:2], T.QI[:, 0:1], 1, None, A.arith_shift_right), e2)
+    done(v.tensor_copy(T.QF[:, 0:1], T.QI[:, 0:1]), e3)
+    for i in range(N):
+        w = float(256 * (i + 6 if source else i))
+        done(v.tensor_scalar(T.SI[:, 128 * i:128 * i + 128], T.IDN[:], w, None, A.mult), cv)
+    need("v", e2)
+    e4 = new()
+    done(v.tensor_copy(T.QF[:, 1:2], T.QI[:, 1:2]), e4)
+    need("v", e3)
+    e5 = new()
+    if source:
+        done(v.tensor_scalar(T.QF[:, 2:3], T.QF[:, 0:1], 1.0, None, A.add), e5)
+    else:
+        done(v.tensor_scalar(T.TC[:], T.K16[:], T.QF[:, 0:1], float(LAND + 1), A.add, A.add), cv)
+        done(v.tensor_scalar(T.TD[:, 0:F], T.K16[:, 0:F], T.QF[:, 0:1], float(R), A.add, A.add), e5)
+    need("v", e4)
+    done(v.tensor_scalar(T.C8[:], T.ROW8[:], T.QF[:, 1:2], None, A.is_equal), cv)
+    need("v", e5)
+    if source:
+        done(v.tensor_scalar(T.SI[:, 128 * N:128 * N + 128], T.IDN[:], T.QF[:, 2:3], None, A.mult), cv)
+        done(v.memset(T.WIN[:, TR:TR + LAND], 0.0), cv)
+    else:
+        done(v.memset(T.WIN[:, 0:R], 0.0), cv)
+    return cg, cv, e5
+
+
+def values_rows(g, T, tk, cv, hi, lo, lo_first):
+    new, done, need, finish = tk
+    ee = new()
+    need("t", cv, hi, lo)
+    done(g.tensor.matmul(T.ps3[:, 0:F], T.PRM[:, 0:128], T.HI[:], True, False), ee)
+    done(g.tensor.matmul(T.ps3[:, 0:F], T.PRM[:, 128:256], T.LO[:], False, True), ee)
+    done(g.tensor.matmul(T.ps3[:, F:2 * F], T.PRM[:, 256:384], T.HI[:], True, False), ee)
+    done(g.tensor.matmul(T.ps3[:, F:2 * F], T.PRM[:, 384:512], T.LO[:], False, True), ee)
+    return ee
+
+
+def spread(g, T, tk, ev, lo, hi):
+    new, done, need, finish = tk
+    for k in range(lo, hi):
+        o = F * (k % 2)
+        done(g.scalar.activation(T.V[:, k:TR:16], T.ps3[:, o:o + F], COPY, scale=T.C8[:, k // 2:k // 2 + 1]), ev)
+
+
+def positions(g, T, tk, masks, cg, cv, codes, between, mid_scalar, after_scan, nm):
+    new, done, need, finish = tk
+    v, s, t = g.vector, g.scalar, g.tensor
+    mev = [new(), new(), new()]
+    for i in range(N):
+        if i == 4:
+            between()
+        done(v.tensor_scalar(T.M[:, F * i:F * i + F], T.CODE[:], float(codes[i]), None, A.is_equal), mev[i // 4])
+    need("v", cv, *mev)
+    sc = new()
+    done(v.tensor_tensor_scan(T.SC[:], T.RS[:], T.M[:, 0:N * F], 0.0, A.mult, A.add), sc)
+    need("t", cg, cv)
+    wi = [i for i in range(N) if nm is not None or i > 0]
+    first = [True]
+
+    def weigh(i):
+        need("t", mev[i // 4])
+        t.matmul(T.ps2[:, 0:F], T.SI[:, 128 * i:128 * i + 128], T.M[:, F * i:F * i + F], first[0], False)
+        first[0] = False
+
+    for i in wi[:5]:
+        weigh(i)
+    b0, b1 = new(), new()
+    need("t", sc)
+    done(t.matmul(T.ps1[:, 0:N], T.TRI[:], T.SC[:, F - 1:N * F:F], True, True), b1)
+    done(t.matmul(T.ps0[:, 0:N], T.TRI[:], T.SC[:, F - 1:N * F:F], True, True), b0)
+    for i in wi[5:]:
+        weigh(i)
+    after_scan()
+    need("s", b1, sc)
+    bs = new()
+    done(s.activation(T.BS[:, 0:N], T.ps1[:, 0:N], COPY), bs)
+    need("s", bs)
+    ts = [new(), new(), new()]
+    for i in range(4, N):
+        done(s.activation(T["ps%d" % (4 + i // 4)][:, F * (i % 4):F * (i % 4) + F], T.SC[:, F * i:F * i + F], IDENT,
+                          bias=T.BS[:, i:i + 1]), ts[i // 4])
+    mid_scalar()
+    need("v", b0, sc)
+    for i in range(4):
+        done(v.tensor_scalar(T.ps4[:, F * i:F * i + F], T.SC[:, F * i:F * i + F], T.ps0[:, i:i + 1], None, A.add), ts[0])
+    pe = [new(), new(), new()]
+    for c in range(3):
+        need("v", ts[c])
+        done(v.tensor_tensor(T.P[:, 4 * F * c:4 * F * c + 4 * F], T.M[:, 4 * F * c:4 * F * c + 4 * F],
+                             T["ps%d" % (4 + c)][:, 0:4 * F], A.mult), pe[c])
+    x = new()
+    if nm is not None:
+        need("t", *nm)
+        t.matmul(T.ps2[:, 0:F], T.IDN[:], T.P[:, F * N:F * N + F], False, False)
+        t.matmul(T.ps2[:, 0:F], T.SI[:, 128 * N:128 * N + 128], T.M[:, F * N:F * N + F], False, False)
+    for i in range(N):
+        need("t", pe[i // 4])
+        inst = t.matmul(T.ps2[:, 0:F], T.IDN[:], T.P[:, F * i:F * i + F], False, i == N - 1)
+    done(inst, x)
+    return x
+
+
+def codes_of(g, T, tk, load_s, load_d, extra):
+    new, done, need, finish = tk
+    v = g.vector
+    e = new()
+    need("v", load_s)
+    done(v.tensor_scalar(T.HS[:], T.S[:], 8, 4080, A.arith_shift_right, A.bitwise_and), e)
+    extra()
+    need("v", load_d)
+    done(v.tensor_scalar(T.GD[:], T.D[:], 12, None, A.arith_shift_right), e)
+    need("v", e)
+    c = new()
+    done(v.tensor_tensor(T.CODE[:], T.HS[:], T.GD[:], A.add), c)
+    return c
+
+
+def load_lists(g, T, tk, waits):
+    new, done, need, finish = tk
+    ls, ld = new(), new()
+    for sem, n in waits:
+        g.sync.wait_ge(sem, n)
+        g.scalar.wait_ge(sem, n)
+    done(g.sync.dma_start(T.S[:], T.Ls[:]), ls, 16)
+    done(g.scalar.dma_start(T.D[:], T.Ld[:]), ld, 16)
+    return ls, ld
+
+
+def send_lists(g, core, T, topo, r, dests, sem):
+    eng = shared_engines(topo, core, dests)
+    h = len(eng) // 2
+    ids = []
+    for d in dests:
+        rid, pid = topo.addr(d, core)
+        ids.append(DstId(rid=rid, pnc=pid))
+    g.remote_dma_fused([
+        RemoteDMATransfer(dst_ids=ids, dma_engine_mask=together(eng[:h]), remote_sem=sem, srcs=[T.Ls[r]], dsts=[T.Ls[r] for d in dests]),
+        RemoteDMATransfer(dst_ids=ids, dma_engine_mask=together(eng[h:]), remote_sem=sem, srcs=[T.Ld[r]], dsts=[T.Ld[r] for d in dests]),
+    ], local_sem=T.sem.ls)
+    return len(eng)
+
+
+def send_block(g, core, T, topo, dest, out, in_, sem):
+    eng = shared_engines(topo, core, [dest])
+    rid, pid = topo.addr(dest, core)
+    g.remote_dma(out, in_, sem, T.sem.ls, pid, rid, together(eng))
+    return len(eng)
+
+
+def source_rank(g, core, T, topo, r):
+    tk = tools(g, T)
+    new, done, need, finish = tk
+    v, s = g.vector, g.scalar
+    peer, diag, far, near, direct = layout(T, topo, r)
+    left = 0
+    pr = new()
+    done(g.sync.dma_start(T.Ls[r], T.src[:]), pr, 16)
+    done(s.dma_start(T.Ld[r], T.dst[:]), pr, 16)
+    cg, cv, e5 = constants(g, T, tk, True)
+    need("g", pr)
+    pc = T.cores[peer]
+    k = send_lists(g, core, T, topo, r, [pc, helper_of(pc, topo)], T.sem.lp)
+    left += k
+    rest = [t for t in direct if t != peer]
+    ds = [T.cores[t] for t in rest] + [helper_of(T.cores[t], topo) for t in rest] + [helper_of(core, topo)]
+    left += send_lists(g, core, T, topo, r, ds, T.sem.la)
+    on = [T.cores[t] for t in layout(T, topo, peer)[1]]
+    g.wait_ge(T.sem.lp, k)
+    left += send_lists(g, core, T, topo, peer, on, T.sem.la)
+    need("y", pr)
+    need("s", pr)
+    load_s, load_d = load_lists(g, T, tk, [(T.sem.lp, k), (T.sem.la, k * (N - 2))])
+    tab = new()
+    need("y", load_s, load_d)
+    done(g.sync.dma_start(T.W[:, LAND:LAND + R], T.tab[:]), tab, 16)
+
+    order = diag + [r] + far + near
+    sl, hi, lo, nm1, nm2 = new(), new(), new(), new(), new()
+
+    def take_sl():
+        done(v.tensor_scalar(T.SL[:], T.S[:], float(-R * r), None, A.add), sl)
+        need("s", sl)
+        done(s.activation(T.HI[:], T.SL[:], COPY), hi)
+
+    code = codes_of(g, T, tk, load_s, load_d, take_sl)
+    need("v", code)
+    vv = new()
+
+    def between():
+        need("v", sl, hi)
+        done(v.tensor_tensor(T.LO[:], T.SL[:], T.HI[:], A.subtract), lo)
+        ee = values_rows(g, T, tk, cv, hi, lo, True)
+        need("s", cv, ee)
+        spread(g, T, tk, vv, 0, 9)
+
+    def after_scan():
+        done(v.tensor_scalar(T.M[:, F * N:F * N + F], T.HS[:], float(16 * r), None, A.not_equal), nm1)
+        need("v", nm1)
+        done(v.tensor_tensor(T.P[:, F * N:F * N + F], T.M[:, F * N:F * N + F], T.K16[:, 0:F], A.mult), nm2)
+
+    x = positions(g, T, tk, None, cg, cv, [16 * r + t for t in order], between,
+                  lambda: spread(g, T, tk, vv, 9, 16), after_scan, (nm1, nm2))
+    o = new()
+    need("v", x)
+    done(v.tensor_scalar(T.O[:], T.ps2[:, 0:F], -1.0, None, A.add), o)
+    need("v", o, vv)
+    win = new()
+    done(v.tensor_copy(T.WIN[:, 0:TR + LAND].indirect(T.O[:, 0:F]), T.V[:]), win)
+    need("t", win)
+    wr = []
+    for c in range(3):
+        e = new()
+        st = TR + 4 * CAPP * c
+        for k in range(16):
+            inst = g.tensor.matmul(T["ps%d" % (4 + c)][:, 0:64], T.SEL[:, 128 * k:128 * k + 128],
+                                   T.WIN[:, st + k:st + 4 * CAPP:16], k == 0, k == 15)
+        done(inst, e)
+        wr.append(e)
+    table = T.W[:, LAND:LAND + R]
+    own = new()
+    sent = {}
+    for c in range(3):
+        need("v", wr[c])
+        go = new()
+        done(v.tensor_copy(T.GO[:, 64 * c:64 * c + 64], T["ps%d" % (4 + c)][:, 0:64]), go)
+        need("v", go, tab)
+        need("s", go, tab)
+        if c == 0:
+            for i in range(4):
+                e = own if i == 3 else new()
+                out = T.W[:, CAPP * r:CAPP * r + CAPP] if i == 3 else T.G[:, CAPP * i:CAPP * i + CAPP]
+                src = table.indirect(T.GO[:, 16 * i:16 * i + 16])
+                if i % 2 == 0:
+                    done(v.tensor_copy(out, src), e)
+                else:
+                    done(s.activation(out, src, COPY), e)
+                sent[i] = e
+        else:
+            e = new()
+            a = 4 * c
+            done(v.tensor_copy(T.G[:, CAPP * a:CAPP * (a + 2)], table.indirect(T.GO[:, 16 * a:16 * a + 32])), e)
+            done(s.activation(T.G[:, CAPP * (a + 2):CAPP * (a + 4)], table.indirect(T.GO[:, 16 * a + 32:16 * a + 64]), COPY), e)
+            sent["c%d" % c] = e
+    ph = helper_of(pc, topo)
+    for i in range(3):
+        need("g", sent[i])
+        left += send_block(g, core, T, topo, ph, T.DG[:, CAPP * i:CAPP * i + CAPP], T.G[:, CAPP * i:CAPP * i + CAPP], T.sem["di%d" % i])
+    for c in (1, 2):
+        need("g", sent["c%d" % c])
+        tg = order[4 * c:4 * c + 4]
+        eng = shared_engines(topo, core, [T.cores[t] for t in tg])
+        n = len(eng) // 4
+        trs = []
+        for j, t in enumerate(tg):
+            rid, pid = topo.addr(T.cores[t], core)
+            a = CAPP * (4 * c + j)
+            trs.append(RemoteDMATransfer(dst_ids=[DstId(rid=rid, pnc=pid)], dma_engine_mask=together(eng[n * j:n * j + n]),
+                                         remote_sem=T.sem.da, srcs=[T.G[:, a:a + CAPP]], dsts=[T.W[:, CAPP * r:CAPP * r + CAPP]]))
+        g.remote_dma_fused(trs, local_sem=T.sem.ls)
+        left += len(eng)
+    arrived = 8 * n + 3 * len(eng)
+    inv = len(inverse_engines(topo, helper_of(core, topo), core))
+    for q in (v, s):
+        q.wait_ge(T.sem.iv, inv)
+        q.wait_ge(T.sem.da, arrived)
+    need("v", own)
+    need("s", own)
+    at = 0
+    yo = new()
+    for j, w in enumerate((512, 512, 768, 768, 768, 768)):
+        src = T.W[:].indirect(T.INV[:, at // 16:(at + w) // 16])
+        e = new()
+        if j % 2 == 0:
+            done(v.tensor_copy(T.Y[:, at:at + w], src), e)
+        else:
+            done(s.activation(T.Y[:, at:at + w], src, COPY), e)
+        need("y", e)
+        done(g.sync.dma_start(T.y[:, at:at + w], T.Y[:, at:at + w]), yo, 16)
+        at += w
+    need("y", yo)
+    g.wait_ge(T.sem.ls, left)
+    finish()
+
+
+def inverse_engines(topo, helper, core):
+    eng = shared_engines(topo, helper, [core])
+    out = [d for d in topo_far(topo, core)]
+    off = shared_engines(topo, helper, out)
+    return [b for b in eng if b not in off] or eng
+
+
+def topo_far(topo, core):
+    for d in range(core % 8, core + 1024, 8):
+        if topo.same_plane(core, d):
+            return [d]
+    return [core]
+
+
+def helper(g, core, T, topo, r):
+    tk = tools(g, T)
+    new, done, need, finish = tk
+    v, s = g.vector, g.scalar
+    peer, diag, far, near, direct = layout(T, topo, r)
+    left = 0
+    cg, cv, e5 = constants(g, T, tk, False)
+    td = new()
+    need("v", e5)
+    done(v.tensor_scalar(T.TD[:, F:2 * F], T.TD[:, 0:F], float(R * r), None, A.add), td)
+    on = layout(T, topo, peer)[1]
+    k = len(shared_engines(topo, core, [T.cores[t] for t in on]))
+    g.wait_ge(T.sem.lp, k)
+    left += send_lists(g, core, T, topo, peer, [helper_of(T.cores[t], topo) for t in on], T.sem.la)
+    load_s, load_d = load_lists(g, T, tk, [(T.sem.lp, k), (T.sem.la, k * (N - 1))])
+    for i, t in enumerate(on):
+        g.wait_ge(T.sem["di%d" % i], k)
+        left += send_block(g, core, T, topo, T.cores[t], T.W[:, CAPP * peer:CAPP * peer + CAPP], T.DG[:, CAPP * i:CAPP * i + CAPP], T.sem.da)
+
+    code = codes_of(g, T, tk, load_s, load_d, lambda: None)
+    need("v", code)
+    o = new()
+
+    def after_scan():
+        a, b, c = new(), new(), new()
+        done(v.tensor_scalar(T.MM[:], T.GD[:], float(r), None, A.is_equal), a)
+        need("v", td)
+        done(v.tensor_tensor(T.U[:, 0:F], T.D[:], T.TD[:, F:2 * F], A.subtract), a)
+        need("v", a)
+        done(v.tensor_tensor(T.U[:, F:2 * F], T.U[:, 0:F], T.MM[:], A.mult), b)
+        need("v", b)
+        done(v.tensor_tensor(T.U[:, 2 * F:3 * F], T.U[:, F:2 * F], T.TD[:, 0:F], A.add), c)
+        need("v", c)
+        done(v.tensor_copy(T.O[:], T.U[:, 2 * F:3 * F]), o)
+
+    x = positions(g, T, tk, None, cg, cv, [16 * h + r for h in range(N)], lambda: None, lambda: None, after_scan, None)
+    hi, lo, vv = new(), new(), new()
+    need("s", x)
+    done(s.activation(T.HI[:], T.ps2[:, 0:F], COPY), hi)
+    need("v", hi, x)
+    done(v.tensor_tensor(T.LO[:], T.ps2[:, 0:F], T.HI[:], A.subtract), lo)
+    ee = values_rows(g, T, tk, cv, hi, lo, False)
+    need("s", cv, ee)
+    spread(g, T, tk, vv, 0, 16)
+    need("v", o, vv)
+    win = new()
+    done(v.tensor_copy(T.WIN[:, 0:R + TR].indirect(T.O[:, 0:F]), T.V[:]), win)
+    need("t", win)
+    n = R // 16
+    pw = new()
+    for k in range(16):
+        inst = g.tensor.matmul(T.ps4[:, 0:n], T.SEL[:, 128 * k:128 * k + 128], T.WIN[:, k:R:16], k == 0, k == 15)
+    done(inst, pw)
+    a, b, c, d = new(), new(), new(), new()
+    need("v", pw)
+    done(v.tensor_scalar(T.EE[:, 0:n], T.ps4[:, 0:n], 0.0, None, A.is_equal), a)
+    need("v", a)
+    done(v.tensor_tensor(T.EE[:, n:2 * n], T.EE[:, 0:n], T.TC[:], A.mult), b)
+    need("v", b)
+    done(v.tensor_tensor(T.EE[:, 2 * n:3 * n], T.EE[:, n:2 * n], T.ps4[:, 0:n], A.add), c)
+    need("v", c)
+    done(v.tensor_scalar(T.INV[:], T.EE[:, 2 * n:3 * n], -1.0, None, A.add), d)
+    need("g", d)
+    eng = inverse_engines(topo, core, T.cores[r])
+    rid, pid = topo.addr(T.cores[r], core)
+    g.remote_dma(T.INV[:], T.INV[:], T.sem.iv, T.sem.ls, pid, rid, together(eng))
+    left += len(eng)
+    g.wait_ge(T.sem.ls, left)
+    finish()
+
+
+def rank_program(g, core, T, topo):
+    for r in range(N):
+        c = T.cores[r]
+        if core == c:
+            source_rank(g, core, T, topo, r)
+            return
+        if core == helper_of(c, topo):
+            helper(g, core, T, topo, r)
+            return

@@ -6,10 +6,12 @@ CAPP = 256
 R = 4096
 L = 1024
 F = N * L // 128
+KC = 4 * F
 LAND = N * CAPP
 TR = 16 * F
+LIFT = 4096.0
 COPY = ActivationFunctionType.Copy
-IDENT = ActivationFunctionType.Identity
+RELU = ActivationFunctionType.Relu
 A = AluOpType
 
 SCRATCH = {
@@ -20,27 +22,29 @@ SCRATCH = {
     "HS": ("sbuf", [128, F], "int32"),
     "GD": ("sbuf", [128, F], "int32"),
     "CODE": ("sbuf", [128, F], "bfloat16"),
-    "M": ("sbuf", [128, (N + 1) * F], "bfloat16"),
+    "M": ("sbuf", [128, N * F], "bfloat16"),
     "SC": ("sbuf", [128, N * F], "bfloat16"),
-    "P": ("sbuf", [128, (N + 1) * F], "bfloat16"),
-    "BS": ("sbuf", [128, 16], "float32"),
+    "P": ("sbuf", [128, N * F], "bfloat16"),
     "SL": ("sbuf", [128, F], "float32"),
     "HI": ("sbuf", [128, F], "bfloat16"),
     "LO": ("sbuf", [128, F], "bfloat16"),
     "V": ("sbuf", [128, TR], "bfloat16"),
+    "MN": ("sbuf", [128, 4 * F], "bfloat16"),
     "O": ("sbuf", [128, F], "uint16"),
     "WIN": ("sbuf", [128, R + TR], "bfloat16"),
     "GO": ("sbuf", [128, LAND // 16], "uint16"),
     "INV": ("sbuf", [128, R // 16], "uint16"),
     "G": ("sbuf", [128, LAND], "bfloat16"),
     "DG": ("sbuf", [128, 3 * CAPP], "bfloat16"),
-    "W": ("sbuf", [128, LAND + R], "bfloat16"),
+    "W": ("sbuf", [128, R + LAND], "bfloat16"),
     "Y": ("sbuf", [128, R], "bfloat16"),
     "ONE": ("sbuf", [128, 128], "bfloat16"),
+    "NEG": ("sbuf", [128, 128], "bfloat16"),
     "IDN": ("sbuf", [128, 128], "bfloat16"),
+    "TR0": ("sbuf", [128, 128], "bfloat16"),
     "TRI": ("sbuf", [128, 128], "bfloat16"),
-    "SI": ("sbuf", [128, (N + 1) * 128], "bfloat16"),
-    "SEL": ("sbuf", [128, 16 * 128], "bfloat16"),
+    "SI": ("sbuf", [128, 2 * 128], "bfloat16"),
+    "SEL": ("sbuf", [128, 128 + 16], "bfloat16"),
     "PRM": ("sbuf", [128, 4 * 128], "bfloat16"),
     "RS": ("sbuf", [128, N * F], "bfloat16"),
     "PI": ("sbuf", [128, 1], "int32"),
@@ -51,13 +55,13 @@ SCRATCH = {
     "C8": ("sbuf", [128, 8], "float32"),
     "TD": ("sbuf", [128, 2 * F], "float32"),
     "TC": ("sbuf", [128, R // 16], "float32"),
+    "EE": ("sbuf", [128, R // 16], "float32"),
     "MM": ("sbuf", [128, F], "float32"),
     "U": ("sbuf", [128, 3 * F], "float32"),
-    "EE": ("sbuf", [128, 3 * R // 16], "float32"),
 }
 for _k in range(8):
     SCRATCH["ps%d" % _k] = ("psum", [128, 512], "float32")
-SEMAPHORES = ["lp", "la", "di0", "di1", "di2", "da", "iv", "ls"] + ["e%d" % _k for _k in range(110)]
+SEMAPHORES = ["lp", "la", "di0", "di1", "di2", "da", "iv", "ls", "tb", "g0", "g1"] + ["e%d" % _k for _k in range(110)]
 
 
 def bits(mask):
@@ -75,10 +79,30 @@ def shared_engines(topo, core, dests):
     return bits(m)
 
 
+def other_chip(topo, core):
+    for d in range(core % 8, core + 1024, 8):
+        if topo.same_plane(core, d):
+            return d
+    return core
+
+
+def inside_engines(topo, core, dest):
+    eng = shared_engines(topo, core, [dest])
+    off = shared_engines(topo, core, [other_chip(topo, core)])
+    return [b for b in eng if b not in off] or eng
+
+
+def chip_cores(c, topo, same_die):
+    return [x for x in range(max(0, c - 7), c + 8)
+            if x != c and topo.host(x) == topo.host(c) and topo.chip(x) == topo.chip(c) and (topo.die(x) == topo.die(c)) == same_die]
+
+
 def helper_of(c, topo):
-    near = [x for x in range(max(0, c - 7), c + 8)
-            if x != c and topo.host(x) == topo.host(c) and topo.chip(x) == topo.chip(c) and topo.die(x) == topo.die(c)]
-    return near[-1]
+    return chip_cores(c, topo, True)[-1]
+
+
+def second_of(c, topo):
+    return chip_cores(c, topo, False)[0]
 
 
 def layout(T, topo, r):
@@ -93,9 +117,9 @@ def layout(T, topo, r):
     diag = diag[turn:] + diag[:turn]
     far = far[turn:] + far[:turn]
     mate = [t for t in near if topo.host(T.cores[t]) != topo.host(c)]
-    same = [t for t in near if t not in mate]
-    near = mate[turn:] + mate[:turn] + same
-    return peer, diag, far, near, direct
+    mate = mate[turn:] + mate[:turn]
+    same = [t for t in near if topo.host(T.cores[t]) == topo.host(c)]
+    return peer, diag, far, mate, same, direct
 
 
 def tools(g, T):
@@ -130,131 +154,149 @@ def tools(g, T):
 
 def constants(g, T, tk, source):
     new, done, need, finish = tk
-    v = g.vector
-    one, z, cg = new(), new(), new()
+    v, s = g.vector, g.scalar
+    one, neg, z, ci, cg, ct = new(), new(), new(), new(), new(), new()
     done(v.memset(T.ONE[:], 1.0), one)
+    done(v.memset(T.NEG[:], -1.0), neg)
     done(v.memset(T.SEL[:], 0.0), z)
     done(v.memset(T.PRM[:], 0.0), z)
     done(v.memset(T.RS[:], 1.0), z)
-    done(g.iota(T.PI[:], [[1, 1]], 0, 1), cg)
-    done(g.iota(T.K16[:], [[16, R // 16]], 0, 0, allow_small_or_imprecise_dtypes=True), cg)
-    done(g.iota(T.ROW8[:], [[1, 8]], 0, 0, allow_small_or_imprecise_dtypes=True), cg)
+    done(g.iota(T.PI[:], [[1, 1]], 0, 1), ci)
+    done(g.iota(T.ROW8[:], [[1, 8]], 0, 0, allow_small_or_imprecise_dtypes=True), ci)
     need("g", one)
-    done(g.affine_select(T.IDN[:], T.ONE[:], [[-1, 128]], A.is_equal, 0.0, 0, 1), cg)
-    done(g.affine_select(T.TRI[:], T.ONE[:], [[1, 128]], A.is_gt, 0.0, 0, -1), cg)
+    done(g.affine_select(T.IDN[:], T.ONE[:], [[-1, 128]], A.is_equal, 0.0, 0, 1), ci)
+
+    def late():
+        n = F if source else R // 16
+        done(g.iota(T.K16[:, 0:n], [[16, n]], -TR if source else 0, 0, allow_small_or_imprecise_dtypes=True), cg)
+        t0 = new()
+        need("g", neg)
+        done(g.affine_select(T.TR0[:], T.NEG[:], [[-1, 128]], A.is_gt, 0.0, 0, 1), t0)
+        need("g", t0)
+        done(g.affine_select(T.TRI[:], T.TR0[:], [[-1, 128]], A.not_equal, LIFT, 0, 1), ct)
+
     cv = new()
     need("v", z)
-    for k in range(16):
-        done(v.memset(T.SEL[:, 128 * k + k:128 * k + 128:16], 1.0), cv)
+    done(v.memset(T.SEL[:, 15:128 + 16:16], 1.0), cv)
     done(v.memset(T.RS[:, 0:N * F:F], 0.0), cv)
-    need("v", cg)
-    e1, e2, e3 = new(), new(), new()
+    need("v", ci)
+    e1, e2, e3, e4 = new(), new(), new(), new()
     done(v.tensor_scalar(T.QI[:, 0:1], T.PI[:], 15, None, A.bitwise_and), e1)
     done(v.tensor_copy(T.PRM[:, 0:128:2], T.IDN[:, 0:128:2]), cv)
-    done(v.tensor_copy(T.PRM[:, 129:256:2], T.IDN[:, 0:128:2]), cv)
-    done(v.tensor_copy(T.PRM[:, 257:384:2], T.IDN[:, 1:128:2]), cv)
-    done(v.tensor_copy(T.PRM[:, 384:512:2], T.IDN[:, 1:128:2]), cv)
     need("v", e1)
     done(v.tensor_scalar(T.QI[:, 1:2], T.QI[:, 0:1], 1, None, A.arith_shift_right), e2)
     done(v.tensor_copy(T.QF[:, 0:1], T.QI[:, 0:1]), e3)
-    for i in range(N):
-        w = float(256 * (i + 6 if source else i))
-        done(v.tensor_scalar(T.SI[:, 128 * i:128 * i + 128], T.IDN[:], w, None, A.mult), cv)
+    done(v.tensor_copy(T.PRM[:, 129:256:2], T.IDN[:, 0:128:2]), cv)
     need("v", e2)
-    e4 = new()
     done(v.tensor_copy(T.QF[:, 1:2], T.QI[:, 1:2]), e4)
-    need("v", e3)
-    e5 = new()
-    if source:
-        done(v.tensor_scalar(T.QF[:, 2:3], T.QF[:, 0:1], 1.0, None, A.add), e5)
-    else:
-        done(v.tensor_scalar(T.TC[:], T.K16[:], T.QF[:, 0:1], float(LAND + 1), A.add, A.add), cv)
-        done(v.tensor_scalar(T.TD[:, 0:F], T.K16[:, 0:F], T.QF[:, 0:1], float(R), A.add, A.add), e5)
+    done(v.tensor_copy(T.PRM[:, 257:384:2], T.IDN[:, 1:128:2]), cv)
     need("v", e4)
     done(v.tensor_scalar(T.C8[:], T.ROW8[:], T.QF[:, 1:2], None, A.is_equal), cv)
-    need("v", e5)
+    done(v.tensor_copy(T.PRM[:, 384:512:2], T.IDN[:, 1:128:2]), cv)
+    si = new()
     if source:
-        done(v.tensor_scalar(T.SI[:, 128 * N:128 * N + 128], T.IDN[:], T.QF[:, 2:3], None, A.mult), cv)
+        need("s", ci, e3)
+        done(s.activation(T.SI[:, 0:128], T.IDN[:], COPY, scale=float(CAPP)), si)
+        done(s.activation(T.SI[:, 128:256], T.IDN[:], COPY, scale=T.QF[:, 0:1]), si)
         done(v.memset(T.WIN[:, TR:TR + LAND], 0.0), cv)
     else:
         done(v.memset(T.WIN[:, 0:R], 0.0), cv)
-    return cg, cv, e5
+    return {"ci": ci, "cg": cg, "ct": ct, "cv": cv, "si": si, "q": e3, "z": z, "one": one, "late": late}
 
 
-def values_rows(g, T, tk, cv, hi, lo, lo_first):
+def sel(T, j):
+    return T.SEL[:, 15 - j:143 - j]
+
+
+def spread(q, T, tk, ev, ks, bank):
     new, done, need, finish = tk
-    ee = new()
-    need("t", cv, hi, lo)
-    done(g.tensor.matmul(T.ps3[:, 0:F], T.PRM[:, 0:128], T.HI[:], True, False), ee)
-    done(g.tensor.matmul(T.ps3[:, 0:F], T.PRM[:, 128:256], T.LO[:], False, True), ee)
-    done(g.tensor.matmul(T.ps3[:, F:2 * F], T.PRM[:, 256:384], T.HI[:], True, False), ee)
-    done(g.tensor.matmul(T.ps3[:, F:2 * F], T.PRM[:, 384:512], T.LO[:], False, True), ee)
-    return ee
+    for j in ks:
+        out, in_, c8 = T.V[:, j:TR:16], bank[j % 2], T.C8[:, j // 2:j // 2 + 1]
+        if q[0] == "s":
+            done(q[1].activation(out, in_, COPY, scale=c8), ev)
+        else:
+            done(q[1].tensor_scalar(out, in_, c8, None, A.mult), ev)
 
 
-def spread(g, T, tk, ev, lo, hi):
-    new, done, need, finish = tk
-    for k in range(lo, hi):
-        o = F * (k % 2)
-        done(g.scalar.activation(T.V[:, k:TR:16], T.ps3[:, o:o + F], COPY, scale=T.C8[:, k // 2:k // 2 + 1]), ev)
-
-
-def positions(g, T, tk, masks, cg, cv, codes, between, mid_scalar, after_scan, nm):
+def numbers(g, T, tk, cs, codes, step, last):
     new, done, need, finish = tk
     v, s, t = g.vector, g.scalar, g.tensor
-    mev = [new(), new(), new()]
-    for i in range(N):
-        if i == 4:
-            between()
-        done(v.tensor_scalar(T.M[:, F * i:F * i + F], T.CODE[:], float(codes[i]), None, A.is_equal), mev[i // 4])
-    need("v", cv, *mev)
-    sc = new()
-    done(v.tensor_tensor_scan(T.SC[:], T.RS[:], T.M[:, 0:N * F], 0.0, A.mult, A.add), sc)
-    need("t", cg, cv)
-    wi = [i for i in range(N) if nm is not None or i > 0]
-    first = [True]
+    mev, tot, scv = [[new() for _ in range(3)] for _ in range(3)]
+    tb = ["ps0", "ps1", "ps0"]
+    parts = [("ps4", 0, KC, "s"), ("ps5", KC, KC, "v"), ("ps6", 2 * KC, KC // 2, "s"), ("ps1", 2 * KC + KC // 2, KC // 2, "v")]
+    sub, pe = [[new() for _ in parts] for _ in range(2)]
+    need("t", cs["one"], cs["z"])
 
-    def weigh(i):
-        need("t", mev[i // 4])
-        t.matmul(T.ps2[:, 0:F], T.SI[:, 128 * i:128 * i + 128], T.M[:, F * i:F * i + F], first[0], False)
-        first[0] = False
+    def masks(c):
+        for i in range(4 * c, 4 * c + 4):
+            done(v.tensor_scalar(T.M[:, F * i:F * i + F], T.CODE[:], float(codes[i]), None, A.is_equal), mev[c])
 
-    for i in wi[:5]:
-        weigh(i)
-    b0, b1 = new(), new()
-    need("t", sc)
-    done(t.matmul(T.ps1[:, 0:N], T.TRI[:], T.SC[:, F - 1:N * F:F], True, True), b1)
-    done(t.matmul(T.ps0[:, 0:N], T.TRI[:], T.SC[:, F - 1:N * F:F], True, True), b0)
-    for i in wi[5:]:
-        weigh(i)
-    after_scan()
-    need("s", b1, sc)
-    bs = new()
-    done(s.activation(T.BS[:, 0:N], T.ps1[:, 0:N], COPY), bs)
-    need("s", bs)
-    ts = [new(), new(), new()]
-    for i in range(4, N):
-        done(s.activation(T["ps%d" % (4 + i // 4)][:, F * (i % 4):F * (i % 4) + F], T.SC[:, F * i:F * i + F], IDENT,
-                          bias=T.BS[:, i:i + 1]), ts[i // 4])
-    mid_scalar()
-    need("v", b0, sc)
-    for i in range(4):
-        done(v.tensor_scalar(T.ps4[:, F * i:F * i + F], T.SC[:, F * i:F * i + F], T.ps0[:, i:i + 1], None, A.add), ts[0])
-    pe = [new(), new(), new()]
-    for c in range(3):
-        need("v", ts[c])
-        done(v.tensor_tensor(T.P[:, 4 * F * c:4 * F * c + 4 * F], T.M[:, 4 * F * c:4 * F * c + 4 * F],
-                             T["ps%d" % (4 + c)][:, 0:4 * F], A.mult), pe[c])
-    x = new()
-    if nm is not None:
-        need("t", *nm)
-        t.matmul(T.ps2[:, 0:F], T.IDN[:], T.P[:, F * N:F * N + F], False, False)
-        t.matmul(T.ps2[:, 0:F], T.SI[:, 128 * N:128 * N + 128], T.M[:, F * N:F * N + F], False, False)
-    for i in range(N):
-        need("t", pe[i // 4])
-        inst = t.matmul(T.ps2[:, 0:F], T.IDN[:], T.P[:, F * i:F * i + F], False, i == N - 1)
-    done(inst, x)
-    return x
+    def totals(c):
+        need("t", mev[c])
+        done(t.matmul(T[tb[c]][:, 0:KC], T.ONE[:], T.M[:, KC * c:KC * c + KC], True, True), tot[c])
+
+    def scan(c):
+        need("v", cs["cv"], tot[c])
+        a = KC * c
+        done(v.tensor_tensor_scan(T.SC[:, a:a + KC], T.RS[:, a:a + KC], T[tb[c]][:, 0:KC], 0.0, A.mult, A.add), scv[c])
+
+    def lower(j):
+        b, a, w, e = parts[j]
+        need("t", cs["ct"])
+        t.matmul(T[b][:, 0:w], T.TRI[:], T.M[:, a:a + w], True, False)
+
+    def take(j):
+        b, a, w, e = parts[j]
+        need("t", cs["ci"], scv[min(j, 2)])
+        done(t.matmul(T[b][:, 0:w], T.IDN[:], T.SC[:, a:a + w], False, True), sub[j])
+
+    def cut(j):
+        b, a, w, e = parts[j]
+        need(e, sub[j])
+        if e == "s":
+            done(s.activation(T.P[:, a:a + w], T[b][:, 0:w], RELU, bias=-LIFT - 1.0), pe[j])
+        else:
+            done(v.tensor_scalar(T.P[:, a:a + w], T[b][:, 0:w], -LIFT - 1.0, 0.0, A.add, A.max), pe[j])
+
+    def add(j, first=False, end=False):
+        b, a, w, e = parts[j]
+        need("t", pe[j])
+        for i in range(a, a + w, F):
+            inst = t.matmul(T.ps7[:, 0:F], T.IDN[:], T.P[:, i:i + F], first and i == a, end and i == a + w - F)
+        if end:
+            done(inst, last)
+
+    masks(0)
+    totals(0)
+    step(0)
+    masks(1)
+    totals(1)
+    lower(0)
+    lower(1)
+    step(1)
+    scan(0)
+    masks(2)
+    need("t", scv[0])
+    totals(2)
+    lower(2)
+    take(0)
+    scan(1)
+    take(1)
+    lower(3)
+    step(2)
+    cut(0)
+    scan(2)
+    take(2)
+    take(3)
+    step(3)
+    cut(1)
+    cut(2)
+    cut(3)
+    add(0, True)
+    step(4)
+    add(1)
+    add(2)
+    add(3, False, True)
 
 
 def codes_of(g, T, tk, load_s, load_d, extra):
@@ -269,7 +311,7 @@ def codes_of(g, T, tk, load_s, load_d, extra):
     need("v", e)
     c = new()
     done(v.tensor_tensor(T.CODE[:], T.HS[:], T.GD[:], A.add), c)
-    return c
+    need("v", c)
 
 
 def load_lists(g, T, tk, waits):
@@ -283,40 +325,81 @@ def load_lists(g, T, tk, waits):
     return ls, ld
 
 
-def send_lists(g, core, T, topo, r, dests, sem):
-    eng = shared_engines(topo, core, dests)
-    h = len(eng) // 2
+def list_transfer(core, T, topo, buf, r, dests, eng, sem):
     ids = []
     for d in dests:
         rid, pid = topo.addr(d, core)
         ids.append(DstId(rid=rid, pnc=pid))
-    g.remote_dma_fused([
-        RemoteDMATransfer(dst_ids=ids, dma_engine_mask=together(eng[:h]), remote_sem=sem, srcs=[T.Ls[r]], dsts=[T.Ls[r] for d in dests]),
-        RemoteDMATransfer(dst_ids=ids, dma_engine_mask=together(eng[h:]), remote_sem=sem, srcs=[T.Ld[r]], dsts=[T.Ld[r] for d in dests]),
-    ], local_sem=T.sem.ls)
+    return RemoteDMATransfer(dst_ids=ids, dma_engine_mask=together(eng), remote_sem=sem, srcs=[buf[r]], dsts=[buf[r] for d in dests])
+
+
+def send_lists(g, core, T, topo, r, dests, sem, dests_d=None):
+    dd = dests_d or dests
+    eng = shared_engines(topo, core, dd)
+    h = len(eng) // 2
+    g.remote_dma_fused([list_transfer(core, T, topo, T.Ls, r, dests, eng[:h], sem),
+                        list_transfer(core, T, topo, T.Ld, r, dd, eng[h:], sem)], local_sem=T.sem.ls)
     return len(eng)
 
 
-def send_block(g, core, T, topo, dest, out, in_, sem):
-    eng = shared_engines(topo, core, [dest])
+def send_list(g, core, T, topo, buf, r, dests, sem):
+    eng = shared_engines(topo, core, dests)
+    g.remote_dma_fused([list_transfer(core, T, topo, buf, r, dests, eng, sem)], local_sem=T.sem.ls)
+    return len(eng)
+
+
+def send_block(g, core, T, topo, dest, out, in_, sem, inside=False):
+    eng = inside_engines(topo, core, dest) if inside else shared_engines(topo, core, [dest])
     rid, pid = topo.addr(dest, core)
     g.remote_dma(out, in_, sem, T.sem.ls, pid, rid, together(eng))
     return len(eng)
+
+
+def landing(T, h):
+    return T.W[:, R + CAPP * h:R + CAPP * h + CAPP]
+
+
+def gather(g, T, tk, ts):
+    new, done, need, finish = tk
+    v, s = g.vector, g.scalar
+    evs = [new() for t in ts]
+
+    def part(q, j, a, w):
+        b = CAPP * ts[j] + a
+        src = T.W[:, 0:R].indirect(T.GO[:, b // 16:(b + w) // 16])
+        if q == "v":
+            done(v.tensor_copy(T.G[:, b:b + w], src), evs[j])
+        else:
+            done(s.activation(T.G[:, b:b + w], src, COPY), evs[j])
+
+    for j in range(len(ts)):
+        if j % 2 == 0 and j == len(ts) - 1:
+            part("v", j, 0, CAPP // 2)
+            part("s", j, CAPP // 2, CAPP // 2)
+        else:
+            part("vs"[j % 2], j, 0, CAPP)
+    return evs
+
+
+def shares(diag, far, mate, same):
+    return [(diag, far), (mate + same[:1], same[1:])]
 
 
 def source_rank(g, core, T, topo, r):
     tk = tools(g, T)
     new, done, need, finish = tk
     v, s = g.vector, g.scalar
-    peer, diag, far, near, direct = layout(T, topo, r)
+    peer, diag, far, mate, same, direct = layout(T, topo, r)
+    sec = second_of(core, topo)
     left = 0
     pr = new()
     done(g.sync.dma_start(T.Ls[r], T.src[:]), pr, 16)
     done(s.dma_start(T.Ld[r], T.dst[:]), pr, 16)
-    cg, cv, e5 = constants(g, T, tk, True)
+    cs = constants(g, T, tk, True)
     need("g", pr)
     pc = T.cores[peer]
-    k = send_lists(g, core, T, topo, r, [pc, helper_of(pc, topo)], T.sem.lp)
+    ph = helper_of(pc, topo)
+    k = send_lists(g, core, T, topo, r, [pc, ph], T.sem.lp, [pc, ph, second_of(pc, topo)])
     left += k
     rest = [t for t in direct if t != peer]
     ds = [T.cores[t] for t in rest] + [helper_of(T.cores[t], topo) for t in rest] + [helper_of(core, topo)]
@@ -324,14 +407,18 @@ def source_rank(g, core, T, topo, r):
     on = [T.cores[t] for t in layout(T, topo, peer)[1]]
     g.wait_ge(T.sem.lp, k)
     left += send_lists(g, core, T, topo, peer, on, T.sem.la)
+    cs["late"]()
     need("y", pr)
     need("s", pr)
     load_s, load_d = load_lists(g, T, tk, [(T.sem.lp, k), (T.sem.la, k * (N - 2))])
-    tab = new()
+    tabs = [new(), new()]
     need("y", load_s, load_d)
-    done(g.sync.dma_start(T.W[:, LAND:LAND + R], T.tab[:]), tab, 16)
+    for j in range(2):
+        a = R // 2 * j
+        done(g.sync.dma_start(T.W[:, a:a + R // 2], T.tab[:, a:a + R // 2]), tabs[j], 16)
+        need("g", tabs[j])
+        left += send_block(g, core, T, topo, sec, T.W[:, a:a + R // 2], T.W[:, a:a + R // 2], T.sem.tb)
 
-    order = diag + [r] + far + near
     sl, hi, lo, nm1, nm2 = new(), new(), new(), new(), new()
 
     def take_sl():
@@ -339,87 +426,78 @@ def source_rank(g, core, T, topo, r):
         need("s", sl)
         done(s.activation(T.HI[:], T.SL[:], COPY), hi)
 
-    code = codes_of(g, T, tk, load_s, load_d, take_sl)
-    need("v", code)
-    vv = new()
+    codes_of(g, T, tk, load_s, load_d, take_sl)
+    vv, ee = new(), new()
+    bank = [T.ps3[:, 0:F], T.ps3[:, F:2 * F]]
+    x, mine, gm = new(), new(), new()
 
-    def between():
-        need("v", sl, hi)
-        done(v.tensor_tensor(T.LO[:], T.SL[:], T.HI[:], A.subtract), lo)
-        ee = values_rows(g, T, tk, cv, hi, lo, True)
-        need("s", cv, ee)
-        spread(g, T, tk, vv, 0, 9)
+    def step(c):
+        if c == 0:
+            need("v", sl, hi)
+            done(v.tensor_tensor(T.LO[:], T.SL[:], T.HI[:], A.subtract), lo)
+            need("t", cs["cv"], hi, lo)
+            for j in range(2):
+                done(g.tensor.matmul(bank[j], T.PRM[:, 256 * j:256 * j + 128], T.HI[:], True, False), ee)
+                done(g.tensor.matmul(bank[j], T.PRM[:, 256 * j + 128:256 * j + 256], T.LO[:], False, True), ee)
+            need("s", cs["cv"], ee)
+            spread(("s", s), T, tk, vv, range(0, 10), bank)
+        if c == 1:
+            done(v.tensor_scalar(T.MN[:, 0:F], T.HS[:], float(16 * r), None, A.is_equal), mine)
+            done(v.tensor_scalar(T.MN[:, F:2 * F], T.HS[:], float(16 * r), None, A.not_equal), nm1)
+        if c == 2:
+            need("v", mine, nm1, cs["cg"])
+            done(v.tensor_tensor(T.MN[:, 2 * F:3 * F], T.MN[:, 0:F], T.GD[:], A.mult), gm)
+        if c == 3:
+            done(v.tensor_tensor(T.MN[:, 3 * F:4 * F], T.MN[:, F:2 * F], T.K16[:, 0:F], A.mult), nm2)
+            spread(("s", s), T, tk, vv, range(10, 16), bank)
+        if c == 4:
+            need("t", cs["si"], nm1, gm, nm2)
+            g.tensor.matmul(T.ps7[:, 0:F], T.SI[:, 0:128], T.MN[:, 2 * F:3 * F], False, False)
+            g.tensor.matmul(T.ps7[:, 0:F], T.SI[:, 128:256], T.MN[:, F:2 * F], False, False)
+            g.tensor.matmul(T.ps7[:, 0:F], T.IDN[:], T.MN[:, 3 * F:4 * F], False, False)
 
-    def after_scan():
-        done(v.tensor_scalar(T.M[:, F * N:F * N + F], T.HS[:], float(16 * r), None, A.not_equal), nm1)
-        need("v", nm1)
-        done(v.tensor_tensor(T.P[:, F * N:F * N + F], T.M[:, F * N:F * N + F], T.K16[:, 0:F], A.mult), nm2)
-
-    x = positions(g, T, tk, None, cg, cv, [16 * r + t for t in order], between,
-                  lambda: spread(g, T, tk, vv, 9, 16), after_scan, (nm1, nm2))
+    numbers(g, T, tk, cs, [16 * r + t for t in range(N)], step, x)
     o = new()
     need("v", x)
-    done(v.tensor_scalar(T.O[:], T.ps2[:, 0:F], -1.0, None, A.add), o)
+    done(v.tensor_scalar(T.O[:], T.ps7[:, 0:F], float(TR), None, A.add), o)
     need("v", o, vv)
     win = new()
     done(v.tensor_copy(T.WIN[:, 0:TR + LAND].indirect(T.O[:, 0:F]), T.V[:]), win)
     need("t", win)
-    wr = []
-    for c in range(3):
-        e = new()
-        st = TR + 4 * CAPP * c
-        for k in range(16):
-            inst = g.tensor.matmul(T["ps%d" % (4 + c)][:, 0:64], T.SEL[:, 128 * k:128 * k + 128],
-                                   T.WIN[:, st + k:st + 4 * CAPP:16], k == 0, k == 15)
-        done(inst, e)
-        wr.append(e)
-    table = T.W[:, LAND:LAND + R]
-    own = new()
-    sent = {}
-    for c in range(3):
+    parts = shares(diag, far, mate, same)
+    first = [min(parts[0][0] + parts[0][1]), min(parts[1][0] + parts[1][1] + [r])]
+    wr, go = [new(), new()], [new(), new()]
+    for c in range(2):
+        st = TR + CAPP * first[c]
+        for j in range(16):
+            inst = g.tensor.matmul(T["ps%d" % (1 + c)][:, 0:F], sel(T, j), T.WIN[:, st + j:st + 16 * F:16], j == 0, j == 15)
+        done(inst, wr[c])
+    n = 0
+    for c in range(2):
+        ours, hers = parts[c]
+        a = 16 * first[c]
         need("v", wr[c])
-        go = new()
-        done(v.tensor_copy(T.GO[:, 64 * c:64 * c + 64], T["ps%d" % (4 + c)][:, 0:64]), go)
-        need("v", go, tab)
-        need("s", go, tab)
-        if c == 0:
-            for i in range(4):
-                e = own if i == 3 else new()
-                out = T.W[:, CAPP * r:CAPP * r + CAPP] if i == 3 else T.G[:, CAPP * i:CAPP * i + CAPP]
-                src = table.indirect(T.GO[:, 16 * i:16 * i + 16])
-                if i % 2 == 0:
-                    done(v.tensor_copy(out, src), e)
-                else:
-                    done(s.activation(out, src, COPY), e)
-                sent[i] = e
-        else:
-            e = new()
-            a = 4 * c
-            done(v.tensor_copy(T.G[:, CAPP * a:CAPP * (a + 2)], table.indirect(T.GO[:, 16 * a:16 * a + 32])), e)
-            done(s.activation(T.G[:, CAPP * (a + 2):CAPP * (a + 4)], table.indirect(T.GO[:, 16 * a + 32:16 * a + 64]), COPY), e)
-            sent["c%d" % c] = e
-    ph = helper_of(pc, topo)
-    for i in range(3):
-        need("g", sent[i])
-        left += send_block(g, core, T, topo, ph, T.DG[:, CAPP * i:CAPP * i + CAPP], T.G[:, CAPP * i:CAPP * i + CAPP], T.sem["di%d" % i])
-    for c in (1, 2):
-        need("g", sent["c%d" % c])
-        tg = order[4 * c:4 * c + 4]
-        eng = shared_engines(topo, core, [T.cores[t] for t in tg])
-        n = len(eng) // 4
-        trs = []
-        for j, t in enumerate(tg):
-            rid, pid = topo.addr(T.cores[t], core)
-            a = CAPP * (4 * c + j)
-            trs.append(RemoteDMATransfer(dst_ids=[DstId(rid=rid, pnc=pid)], dma_engine_mask=together(eng[n * j:n * j + n]),
-                                         remote_sem=T.sem.da, srcs=[T.G[:, a:a + CAPP]], dsts=[T.W[:, CAPP * r:CAPP * r + CAPP]]))
-        g.remote_dma_fused(trs, local_sem=T.sem.ls)
-        left += len(eng)
-    arrived = 8 * n + 3 * len(eng)
-    inv = len(inverse_engines(topo, helper_of(core, topo), core))
+        done(v.tensor_copy(T.GO[:, a:a + F], T["ps%d" % (1 + c)][:, 0:F]), go[c])
+        need("g", go[c])
+        b, w = 16 * min(hers), 16 * len(hers)
+        left += send_block(g, core, T, topo, sec, T.GO[:, b:b + w], T.GO[:, b:b + w], T.sem["g%d" % c], True)
+        need("v", go[c], *tabs)
+        need("s", go[c], *tabs)
+        evs = gather(g, T, tk, ours)
+        for i, t in enumerate(ours):
+            need("g", evs[i])
+            blk = T.G[:, CAPP * t:CAPP * t + CAPP]
+            if c == 0:
+                n = send_block(g, core, T, topo, ph, T.DG[:, CAPP * i:CAPP * i + CAPP], blk, T.sem["di%d" % i])
+            else:
+                n = send_block(g, core, T, topo, T.cores[t], landing(T, r), blk, T.sem.da)
+            left += n
+    own = new()
+    done(v.tensor_copy(landing(T, r), T.W[:, 0:R].indirect(T.GO[:, 16 * r:16 * r + 16])), own)
+    inv = len(inside_engines(topo, helper_of(core, topo), core))
     for q in (v, s):
         q.wait_ge(T.sem.iv, inv)
-        q.wait_ge(T.sem.da, arrived)
+        q.wait_ge(T.sem.da, n * (N - 1))
     need("v", own)
     need("s", own)
     at = 0
@@ -439,87 +517,110 @@ def source_rank(g, core, T, topo, r):
     finish()
 
 
-def inverse_engines(topo, helper, core):
-    eng = shared_engines(topo, helper, [core])
-    out = [d for d in topo_far(topo, core)]
-    off = shared_engines(topo, helper, out)
-    return [b for b in eng if b not in off] or eng
-
-
-def topo_far(topo, core):
-    for d in range(core % 8, core + 1024, 8):
-        if topo.same_plane(core, d):
-            return [d]
-    return [core]
+def second(g, core, T, topo, r):
+    tk = tools(g, T)
+    new, done, need, finish = tk
+    peer, diag, far, mate, same, direct = layout(T, topo, r)
+    on = [helper_of(T.cores[t], topo) for t in layout(T, topo, peer)[1]]
+    g.wait_ge(T.sem.lp, len(shared_engines(topo, T.cores[peer], [core])) // 2)
+    left = send_list(g, core, T, topo, T.Ld, peer, on, T.sem.la)
+    rank = T.cores[r]
+    tab = 2 * len(shared_engines(topo, rank, [core]))
+    for c, (ours, hers) in enumerate(shares(diag, far, mate, same)):
+        for q in (g.vector, g.scalar):
+            if c == 0:
+                q.wait_ge(T.sem.tb, tab)
+            q.wait_ge(T.sem["g%d" % c], len(inside_engines(topo, rank, core)))
+        evs = gather(g, T, tk, hers)
+        for i, t in enumerate(hers):
+            need("g", evs[i])
+            left += send_block(g, core, T, topo, T.cores[t], landing(T, r), T.G[:, CAPP * t:CAPP * t + CAPP], T.sem.da)
+    g.wait_ge(T.sem.ls, left)
+    finish()
 
 
 def helper(g, core, T, topo, r):
     tk = tools(g, T)
     new, done, need, finish = tk
     v, s = g.vector, g.scalar
-    peer, diag, far, near, direct = layout(T, topo, r)
+    peer, diag, far, mate, same, direct = layout(T, topo, r)
     left = 0
-    cg, cv, e5 = constants(g, T, tk, False)
-    td = new()
-    need("v", e5)
-    done(v.tensor_scalar(T.TD[:, F:2 * F], T.TD[:, 0:F], float(R * r), None, A.add), td)
+    cs = constants(g, T, tk, False)
+    cs["late"]()
+    td, tc = [new(), new()], new()
+    need("v", cs["cg"], cs["q"])
+    done(v.tensor_scalar(T.TD[:, 0:F], T.K16[:, 0:F], T.QF[:, 0:1], float(R), A.add, A.add), td[0])
+    done(v.tensor_scalar(T.TC[:], T.K16[:], T.QF[:, 0:1], None, A.add), tc)
+    need("v", td[0])
+    done(v.tensor_scalar(T.TD[:, F:2 * F], T.TD[:, 0:F], float(R * r), None, A.add), td[1])
     on = layout(T, topo, peer)[1]
-    k = len(shared_engines(topo, core, [T.cores[t] for t in on]))
-    g.wait_ge(T.sem.lp, k)
-    left += send_lists(g, core, T, topo, peer, [helper_of(T.cores[t], topo) for t in on], T.sem.la)
-    load_s, load_d = load_lists(g, T, tk, [(T.sem.lp, k), (T.sem.la, k * (N - 1))])
-    for i, t in enumerate(on):
-        g.wait_ge(T.sem["di%d" % i], k)
-        left += send_block(g, core, T, topo, T.cores[t], T.W[:, CAPP * peer:CAPP * peer + CAPP], T.DG[:, CAPP * i:CAPP * i + CAPP], T.sem.da)
+    ne = len(shared_engines(topo, core, [T.cores[t] for t in on]))
+    g.wait_ge(T.sem.lp, ne)
+    left += send_list(g, core, T, topo, T.Ls, peer, [helper_of(T.cores[t], topo) for t in on], T.sem.la)
+    load_s, load_d = load_lists(g, T, tk, [(T.sem.lp, ne), (T.sem.la, ne * (N - 1) + ne * len(diag))])
 
-    code = codes_of(g, T, tk, load_s, load_d, lambda: None)
-    need("v", code)
-    o = new()
+    def pass_on(i):
+        g.wait_ge(T.sem["di%d" % i], ne)
+        return send_block(g, core, T, topo, T.cores[on[i]], landing(T, peer), T.DG[:, CAPP * i:CAPP * i + CAPP], T.sem.da)
 
-    def after_scan():
-        a, b, c = new(), new(), new()
-        done(v.tensor_scalar(T.MM[:], T.GD[:], float(r), None, A.is_equal), a)
-        need("v", td)
-        done(v.tensor_tensor(T.U[:, 0:F], T.D[:], T.TD[:, F:2 * F], A.subtract), a)
-        need("v", a)
-        done(v.tensor_tensor(T.U[:, F:2 * F], T.U[:, 0:F], T.MM[:], A.mult), b)
-        need("v", b)
-        done(v.tensor_tensor(T.U[:, 2 * F:3 * F], T.U[:, F:2 * F], T.TD[:, 0:F], A.add), c)
-        need("v", c)
-        done(v.tensor_copy(T.O[:], T.U[:, 2 * F:3 * F]), o)
+    left += pass_on(0)
+    left += pass_on(1)
 
-    x = positions(g, T, tk, None, cg, cv, [16 * h + r for h in range(N)], lambda: None, lambda: None, after_scan, None)
-    hi, lo, vv = new(), new(), new()
+    codes_of(g, T, tk, load_s, load_d, lambda: None)
+    a, h0, hi, b, c, o, oo = new(), new(), new(), new(), new(), new(), new()
+    x, lo, ee, vv = new(), new(), [new(), new()], new()
+    bank = [T.ps3[:, 0:F], T.ps2[:, 0:F]]
+
+    def step(ch):
+        if ch == 0:
+            done(v.tensor_scalar(T.MM[:], T.GD[:], float(r), None, A.is_equal), a)
+            done(v.tensor_scalar(T.SL[:], T.HS[:], float(CAPP // 16), float(R), A.mult, A.add), h0)
+        if ch == 1:
+            need("v", a, h0)
+            done(v.tensor_tensor(T.HI[:], T.SL[:], T.MM[:], A.mult), hi)
+        if ch == 2:
+            need("v", *td)
+            done(v.tensor_tensor(T.U[:, 0:F], T.D[:], T.TD[:, F:2 * F], A.subtract), b)
+
+    numbers(g, T, tk, cs, [16 * h + r for h in range(N)], step, x)
     need("s", x)
-    done(s.activation(T.HI[:], T.ps2[:, 0:F], COPY), hi)
-    need("v", hi, x)
-    done(v.tensor_tensor(T.LO[:], T.ps2[:, 0:F], T.HI[:], A.subtract), lo)
-    ee = values_rows(g, T, tk, cv, hi, lo, False)
-    need("s", cv, ee)
-    spread(g, T, tk, vv, 0, 16)
-    need("v", o, vv)
+    done(s.activation(T.LO[:], T.ps7[:, 0:F], COPY), lo)
+    need("t", cs["cv"], hi)
+    for j in range(2):
+        g.tensor.matmul(bank[j], T.PRM[:, 256 * j:256 * j + 128], T.HI[:], True, False)
+    need("t", lo)
+    for j in range(2):
+        done(g.tensor.matmul(bank[j], T.PRM[:, 256 * j + 128:256 * j + 256], T.LO[:], False, True), ee[j])
+    need("v", a, b)
+    done(v.tensor_tensor(T.U[:, F:2 * F], T.U[:, 0:F], T.MM[:], A.mult), c)
+    need("v", c)
+    done(v.tensor_tensor(T.U[:, 2 * F:3 * F], T.U[:, F:2 * F], T.TD[:, 0:F], A.add), o)
+    need("v", o)
+    done(v.tensor_copy(T.O[:], T.U[:, 2 * F:3 * F]), oo)
+    need("s", cs["cv"], ee[0])
+    spread(("s", s), T, tk, vv, range(0, 16, 2), bank)
+    need("v", ee[1])
+    spread(("v", v), T, tk, vv, range(1, 16, 2), bank)
+    need("v", oo, vv)
     win = new()
     done(v.tensor_copy(T.WIN[:, 0:R + TR].indirect(T.O[:, 0:F]), T.V[:]), win)
     need("t", win)
-    n = R // 16
-    pw = new()
-    for k in range(16):
-        inst = g.tensor.matmul(T.ps4[:, 0:n], T.SEL[:, 128 * k:128 * k + 128], T.WIN[:, k:R:16], k == 0, k == 15)
-    done(inst, pw)
-    a, b, c, d = new(), new(), new(), new()
-    need("v", pw)
-    done(v.tensor_scalar(T.EE[:, 0:n], T.ps4[:, 0:n], 0.0, None, A.is_equal), a)
-    need("v", a)
-    done(v.tensor_tensor(T.EE[:, n:2 * n], T.EE[:, 0:n], T.TC[:], A.mult), b)
-    need("v", b)
-    done(v.tensor_tensor(T.EE[:, 2 * n:3 * n], T.EE[:, n:2 * n], T.ps4[:, 0:n], A.add), c)
-    need("v", c)
-    done(v.tensor_scalar(T.INV[:], T.EE[:, 2 * n:3 * n], -1.0, None, A.add), d)
+    n = R // 32
+    d = new()
+    for half in range(2):
+        pw, ej = new(), new()
+        ps = T["ps%d" % (4 + half)][:, 0:n]
+        for j in range(16):
+            inst = g.tensor.matmul(ps, sel(T, j), T.WIN[:, R // 2 * half + j:R // 2 * (half + 1):16], j == 0, j == 15)
+        done(inst, pw)
+        at = n * half
+        need("v", pw, tc)
+        done(v.tensor_tensor(T.EE[:, at:at + n], T.TC[:, at:at + n], ps, A.max), ej)
+        need("v", ej)
+        done(v.tensor_copy(T.INV[:, at:at + n], T.EE[:, at:at + n]), d)
     need("g", d)
-    eng = inverse_engines(topo, core, T.cores[r])
-    rid, pid = topo.addr(T.cores[r], core)
-    g.remote_dma(T.INV[:], T.INV[:], T.sem.iv, T.sem.ls, pid, rid, together(eng))
-    left += len(eng)
+    left += send_block(g, core, T, topo, T.cores[r], T.INV[:], T.INV[:], T.sem.iv, True)
+    left += pass_on(2)
     g.wait_ge(T.sem.ls, left)
     finish()
 
@@ -532,4 +633,7 @@ def rank_program(g, core, T, topo):
             return
         if core == helper_of(c, topo):
             helper(g, core, T, topo, r)
+            return
+        if core == second_of(c, topo):
+            second(g, core, T, topo, r)
             return

@@ -5,63 +5,79 @@ N = 12
 CAPP = 256
 R = 4096
 L = 1024
-F = N * L // 128
-KC = 4 * F
+NL = N // 2
+F = NL * L // 128
+KW = F + 1
+CW = 4 * KW + 1
 LAND = N * CAPP
 TR = 16 * F
-LIFT = 4096.0
+BC = CAPP // 8
+NB = 7
+PARTS = [(0, 3), (3, NB)]
 COPY = ActivationFunctionType.Copy
 RELU = ActivationFunctionType.Relu
 A = AluOpType
 
 SCRATCH = {
-    "Ls": ("dram", [N, 128, L // 128], "int32"),
-    "Ld": ("dram", [N, 128, L // 128], "int32"),
+    "Ls": ("dram", [NL, 128, L // 128], "int32"),
+    "Ld": ("dram", [NL, 128, L // 128], "int32"),
+    "Ps": ("dram", [1, 128, L // 128], "int32"),
+    "Pd": ("dram", [1, 128, L // 128], "int32"),
     "S": ("sbuf", [128, F], "int32"),
     "D": ("sbuf", [128, F], "int32"),
     "HS": ("sbuf", [128, F], "int32"),
     "GD": ("sbuf", [128, F], "int32"),
     "CODE": ("sbuf", [128, F], "bfloat16"),
-    "M": ("sbuf", [128, N * F], "bfloat16"),
-    "SC": ("sbuf", [128, N * F], "bfloat16"),
+    "MA": ("sbuf", [128, 3 * CW], "bfloat16"),
+    "MB": ("sbuf", [128, 3 * CW], "bfloat16"),
+    "Z": ("sbuf", [128, 3 * CW], "bfloat16"),
     "P": ("sbuf", [128, N * F], "bfloat16"),
+    "BASE": ("sbuf", [128, N], "float32"),
     "SL": ("sbuf", [128, F], "float32"),
     "HI": ("sbuf", [128, F], "bfloat16"),
     "LO": ("sbuf", [128, F], "bfloat16"),
     "V": ("sbuf", [128, TR], "bfloat16"),
-    "MN": ("sbuf", [128, 4 * F], "bfloat16"),
+    "NM": ("sbuf", [128, F], "bfloat16"),
+    "NK": ("sbuf", [128, F], "bfloat16"),
     "O": ("sbuf", [128, F], "uint16"),
     "WIN": ("sbuf", [128, R + TR], "bfloat16"),
-    "GO": ("sbuf", [128, LAND // 16], "uint16"),
+    "RO": ("sbuf", [128, NB * BC], "bfloat16"),
+    "RX": ("sbuf", [128, NB * BC], "bfloat16"),
+    "RI": ("sbuf", [128, NB * BC], "bfloat16"),
+    "RH": ("sbuf", [128, 512], "bfloat16"),
+    "RA": ("sbuf", [128, 512], "bfloat16"),
+    "RB": ("sbuf", [128, 512], "bfloat16"),
+    "GO": ("sbuf", [128, NB * 16], "uint16"),
     "INV": ("sbuf", [128, R // 16], "uint16"),
-    "G": ("sbuf", [128, LAND], "bfloat16"),
+    "G": ("sbuf", [128, NB * CAPP], "bfloat16"),
     "DG": ("sbuf", [128, 3 * CAPP], "bfloat16"),
+    "FW": ("sbuf", [128, CAPP], "bfloat16"),
     "W": ("sbuf", [128, R + LAND], "bfloat16"),
     "Y": ("sbuf", [128, R], "bfloat16"),
     "ONE": ("sbuf", [128, 128], "bfloat16"),
     "NEG": ("sbuf", [128, 128], "bfloat16"),
     "IDN": ("sbuf", [128, 128], "bfloat16"),
-    "TR0": ("sbuf", [128, 128], "bfloat16"),
+    "NID": ("sbuf", [128, 128], "bfloat16"),
     "TRI": ("sbuf", [128, 128], "bfloat16"),
-    "SI": ("sbuf", [128, 2 * 128], "bfloat16"),
-    "SEL": ("sbuf", [128, 128 + 16], "bfloat16"),
+    "NTI": ("sbuf", [128, 128], "bfloat16"),
+    "DI": ("sbuf", [128, N * 128], "bfloat16"),
+    "DQ": ("sbuf", [128, 128], "bfloat16"),
     "PRM": ("sbuf", [128, 4 * 128], "bfloat16"),
-    "RS": ("sbuf", [128, N * F], "bfloat16"),
+    "L16": ("sbuf", [128, 128], "bfloat16"),
+    "MK": ("sbuf", [128, 128], "bfloat16"),
+    "REP": ("sbuf", [128, 16], "bfloat16"),
     "PI": ("sbuf", [128, 1], "int32"),
-    "QI": ("sbuf", [128, 2], "int32"),
-    "QF": ("sbuf", [128, 4], "float32"),
-    "K16": ("sbuf", [128, R // 16], "float32"),
-    "ROW8": ("sbuf", [128, 8], "float32"),
-    "C8": ("sbuf", [128, 8], "float32"),
-    "TD": ("sbuf", [128, 2 * F], "float32"),
+    "QI": ("sbuf", [128, 4], "int32"),
+    "QF": ("sbuf", [128, 14], "float32"),
+    "ROWS": ("sbuf", [128, 280], "float32"),
+    "K16": ("sbuf", [128, F], "float32"),
     "TC": ("sbuf", [128, R // 16], "float32"),
     "EE": ("sbuf", [128, R // 16], "float32"),
-    "MM": ("sbuf", [128, F], "float32"),
-    "U": ("sbuf", [128, 3 * F], "float32"),
+    "U": ("sbuf", [128, 6 * F], "float32"),
 }
 for _k in range(8):
     SCRATCH["ps%d" % _k] = ("psum", [128, 512], "float32")
-SEMAPHORES = ["lp", "la", "di0", "di1", "di2", "da", "iv", "ls", "tb", "g0", "g1"] + ["e%d" % _k for _k in range(110)]
+SEMAPHORES = ["lp", "la", "di0", "di1", "di2", "da", "iv", "ls", "tb", "fw", "xs0", "xs1"] + ["e%d" % _k for _k in range(100)]
 
 
 def bits(mask):
@@ -86,10 +102,8 @@ def other_chip(topo, core):
     return core
 
 
-def inside_engines(topo, core, dest):
-    eng = shared_engines(topo, core, [dest])
-    off = shared_engines(topo, core, [other_chip(topo, core)])
-    return [b for b in eng if b not in off] or eng
+def leaving_engines(topo, core):
+    return shared_engines(topo, core, [other_chip(topo, core)])
 
 
 def chip_cores(c, topo, same_die):
@@ -98,11 +112,27 @@ def chip_cores(c, topo, same_die):
 
 
 def helper_of(c, topo):
-    return chip_cores(c, topo, True)[-1]
+    return chip_cores(c, topo, True)[0]
 
 
 def second_of(c, topo):
     return chip_cores(c, topo, False)[0]
+
+
+def other_helper_of(c, topo):
+    return chip_cores(c, topo, False)[-1]
+
+
+def rack_of(T, topo, r):
+    return topo.rack(topo.host(T.cores[r]))
+
+
+def slot_of(T, topo, r):
+    return [t for t in range(N) if rack_of(T, topo, t) == rack_of(T, topo, r)].index(r)
+
+
+def downwards(T, topo, r, own):
+    return (rack_of(T, topo, r) == rack_of(T, topo, 0)) != own
 
 
 def layout(T, topo, r):
@@ -110,7 +140,7 @@ def layout(T, topo, r):
     others = [t for t in range(N) if t != r]
     direct = [t for t in others if topo.may_write(c, T.cores[t])]
     diag = [t for t in others if t not in direct]
-    far = [t for t in direct if topo.rack(topo.host(T.cores[t])) != topo.rack(topo.host(c))]
+    far = [t for t in direct if rack_of(T, topo, t) != rack_of(T, topo, r)]
     peer = [t for t in far if topo.chip(T.cores[t]) == topo.chip(c)][0]
     near = [t for t in direct if t not in far]
     turn = r % 3
@@ -119,7 +149,11 @@ def layout(T, topo, r):
     mate = [t for t in near if topo.host(T.cores[t]) != topo.host(c)]
     mate = mate[turn:] + mate[:turn]
     same = [t for t in near if topo.host(T.cores[t]) == topo.host(c)]
-    return peer, diag, far, mate, same, direct
+    return peer, diag, far, mate, same
+
+
+def diag_sender(i, first, second):
+    return first if i == 0 else second
 
 
 def tools(g, T):
@@ -152,151 +186,160 @@ def tools(g, T):
     return new, done, need, finish
 
 
-def constants(g, T, tk, source):
+def constants(g, T, tk, source, down):
     new, done, need, finish = tk
     v, s = g.vector, g.scalar
-    one, neg, z, ci, cg, ct = new(), new(), new(), new(), new(), new()
+    one, z, ci, cv, ct, cm = new(), new(), new(), new(), new(), new()
     done(v.memset(T.ONE[:], 1.0), one)
-    done(v.memset(T.NEG[:], -1.0), neg)
-    done(v.memset(T.SEL[:], 0.0), z)
+    done(v.memset(T.NEG[:], -1.0), one)
     done(v.memset(T.PRM[:], 0.0), z)
-    done(v.memset(T.RS[:], 1.0), z)
+    done(v.memset(T.ROWS[:, 0:16], 0.0), z)
     done(g.iota(T.PI[:], [[1, 1]], 0, 1), ci)
-    done(g.iota(T.ROW8[:], [[1, 8]], 0, 0, allow_small_or_imprecise_dtypes=True), ci)
+    done(g.iota(T.ROWS[:, 16:24], [[1, 8]], 0, 0, allow_small_or_imprecise_dtypes=True), ci)
     need("g", one)
     done(g.affine_select(T.IDN[:], T.ONE[:], [[-1, 128]], A.is_equal, 0.0, 0, 1), ci)
-
-    def late():
-        n = F if source else R // 16
-        done(g.iota(T.K16[:, 0:n], [[16, n]], -TR if source else 0, 0, allow_small_or_imprecise_dtypes=True), cg)
-        t0 = new()
-        need("g", neg)
-        done(g.affine_select(T.TR0[:], T.NEG[:], [[-1, 128]], A.is_gt, 0.0, 0, 1), t0)
-        need("g", t0)
-        done(g.affine_select(T.TRI[:], T.TR0[:], [[-1, 128]], A.not_equal, LIFT, 0, 1), ct)
-
-    cv = new()
+    for c in range(3):
+        done(v.memset(T.MA[:, CW * c:CW * c + CW:KW], 256.0), cv)
+    done(v.memset(T.MB[:, 0:3 * CW:CW], 0.0), cv)
     need("v", z)
-    done(v.memset(T.SEL[:, 15:128 + 16:16], 1.0), cv)
-    done(v.memset(T.RS[:, 0:N * F:F], 0.0), cv)
+    e0, e1, q = new(), new(), new()
+    done(v.memset(T.ROWS[:, 1:16:2], 1.0), e0)
     need("v", ci)
-    e1, e2, e3, e4 = new(), new(), new(), new()
     done(v.tensor_scalar(T.QI[:, 0:1], T.PI[:], 15, None, A.bitwise_and), e1)
-    done(v.tensor_copy(T.PRM[:, 0:128:2], T.IDN[:, 0:128:2]), cv)
+    done(v.tensor_scalar(T.QI[:, 2:3], T.PI[:], 4, None, A.arith_shift_right), e1)
+    done(v.tensor_scalar(T.QI[:, 3:4], T.PI[:], 1, None, A.bitwise_and), e1)
+    done(v.tensor_scalar(T.QI[:, 1:2], T.PI[:], 1, 7, A.arith_shift_right, A.bitwise_and), e1)
+    done(v.tensor_scalar(T.QF[:, 5:6], T.PI[:], -1.0, -1.0, A.mult, A.add), cv)
     need("v", e1)
-    done(v.tensor_scalar(T.QI[:, 1:2], T.QI[:, 0:1], 1, None, A.arith_shift_right), e2)
-    done(v.tensor_copy(T.QF[:, 0:1], T.QI[:, 0:1]), e3)
+    done(v.tensor_copy(T.QF[:, 0:4], T.QI[:]), q)
+    done(v.tensor_copy(T.PRM[:, 0:128:2], T.IDN[:, 0:128:2]), cv)
     done(v.tensor_copy(T.PRM[:, 129:256:2], T.IDN[:, 0:128:2]), cv)
-    need("v", e2)
-    done(v.tensor_copy(T.QF[:, 1:2], T.QI[:, 1:2]), e4)
     done(v.tensor_copy(T.PRM[:, 257:384:2], T.IDN[:, 1:128:2]), cv)
-    need("v", e4)
-    done(v.tensor_scalar(T.C8[:], T.ROW8[:], T.QF[:, 1:2], None, A.is_equal), cv)
     done(v.tensor_copy(T.PRM[:, 384:512:2], T.IDN[:, 1:128:2]), cv)
+    need("v", e0, q)
+    done(v.tensor_scalar(T.QF[:, 6:14], T.ROWS[:, 16:24], T.QF[:, 1:2], None, A.is_equal), cv)
+    done(v.tensor_scalar(T.REP[:], T.ROWS[:, 0:16], T.QF[:, 3:4], None, A.is_equal), cv)
     si = new()
     if source:
-        need("s", ci, e3)
-        done(s.activation(T.SI[:, 0:128], T.IDN[:], COPY, scale=float(CAPP)), si)
-        done(s.activation(T.SI[:, 128:256], T.IDN[:], COPY, scale=T.QF[:, 0:1]), si)
+        if down:
+            done(v.tensor_scalar(T.NID[:], T.IDN[:], -1.0, None, A.mult), cv)
+        qt = new()
+        done(v.tensor_scalar(T.QF[:, 4:5], T.QF[:, 0:1], -255.0 if down else 0.0, None, A.add), qt)
+        need("s", ci, qt)
+        done(s.activation(T.DQ[:], T.IDN[:], COPY, scale=T.QF[:, 4:5]), si)
+        for t in range(1, N):
+            done(s.activation(T.DI[:, 128 * t:128 * t + 128], T.IDN[:], COPY, scale=float(t)), si)
         done(v.memset(T.WIN[:, TR:TR + LAND], 0.0), cv)
     else:
         done(v.memset(T.WIN[:, 0:R], 0.0), cv)
-    return {"ci": ci, "cg": cg, "ct": ct, "cv": cv, "si": si, "q": e3, "z": z, "one": one, "late": late}
 
+    def late():
+        cg, r16 = new(), new()
+        done(g.affine_select(T.TRI[:], T.ONE[:], [[1, 128]], A.is_gt, 0.0, 0, -1), ct)
+        done(g.affine_select(T.NTI[:], T.NEG[:], [[1, 128]], A.is_ge, 0.0, 0, -1), ct)
+        done(g.iota(T.K16[:], [[16, F]], -TR if source else R, 0, allow_small_or_imprecise_dtypes=True), cg)
+        if source:
+            done(g.iota(T.ROWS[:, 24:152], [[0, 8], [1, 16]], 0, 0, allow_small_or_imprecise_dtypes=True), r16)
+        done(g.iota(T.ROWS[:, 152:280], [[0, 8], [1, 8], [0, 2]], 0, 0, allow_small_or_imprecise_dtypes=True), r16)
+        need("v", r16)
+        if source:
+            done(v.tensor_scalar(T.L16[:], T.ROWS[:, 24:152], T.QF[:, 0:1], None, A.is_equal), cm)
+        done(v.tensor_scalar(T.MK[:], T.ROWS[:, 152:280], T.QF[:, 2:3], None, A.is_equal), cm)
+        return cg
 
-def sel(T, j):
-    return T.SEL[:, 15 - j:143 - j]
+    return {"ci": ci, "ct": ct, "cv": cv, "cm": cm, "si": si, "q": q, "late": late}
 
 
 def spread(q, T, tk, ev, ks, bank):
     new, done, need, finish = tk
     for j in ks:
-        out, in_, c8 = T.V[:, j:TR:16], bank[j % 2], T.C8[:, j // 2:j // 2 + 1]
+        out, in_, c8 = T.V[:, j:TR:16], bank[j % 2], T.QF[:, 6 + j // 2:7 + j // 2]
         if q[0] == "s":
             done(q[1].activation(out, in_, COPY, scale=c8), ev)
         else:
             done(q[1].tensor_scalar(out, in_, c8, None, A.mult), ev)
 
 
-def numbers(g, T, tk, cs, codes, step, last):
+def numbers(g, T, tk, cs, codes, lhs, share, step, last, kinds):
     new, done, need, finish = tk
     v, s, t = g.vector, g.scalar, g.tensor
-    mev, tot, scv = [[new() for _ in range(3)] for _ in range(3)]
-    tb = ["ps0", "ps1", "ps0"]
-    parts = [("ps4", 0, KC, "s"), ("ps5", KC, KC, "v"), ("ps6", 2 * KC, KC // 2, "s"), ("ps1", 2 * KC + KC // 2, KC // 2, "v")]
-    sub, pe = [[new() for _ in parts] for _ in range(2)]
-    need("t", cs["one"], cs["z"])
+    me, be, ze, pe, bs, ce = [[new() for _ in range(3)] for _ in range(6)]
 
     def masks(c):
-        for i in range(4 * c, 4 * c + 4):
-            done(v.tensor_scalar(T.M[:, F * i:F * i + F], T.CODE[:], float(codes[i]), None, A.is_equal), mev[c])
+        for j in range(4):
+            a = CW * c + KW * j + 1
+            done(v.tensor_scalar(T.MA[:, a:a + F], T.CODE[:], float(codes[4 * c + j]), 256.0, A.is_equal, A.mult), me[c])
 
-    def totals(c):
-        need("t", mev[c])
-        done(t.matmul(T[tb[c]][:, 0:KC], T.ONE[:], T.M[:, KC * c:KC * c + KC], True, True), tot[c])
+    def behind(c):
+        need("s", cs["cv"], me[c])
+        a = CW * c
+        done(s.activation(T.MB[:, a + 1:a + CW], T.MA[:, a:a + CW - 1], COPY, scale=-255.0 / 256.0), be[c])
+        if kinds:
+            kinds(c, me[c])
 
     def scan(c):
-        need("v", cs["cv"], tot[c])
-        a = KC * c
-        done(v.tensor_tensor_scan(T.SC[:, a:a + KC], T.RS[:, a:a + KC], T[tb[c]][:, 0:KC], 0.0, A.mult, A.add), scv[c])
+        need("v", cs["cv"], me[c], be[c])
+        a = CW * c
+        done(v.tensor_tensor_scan(T.Z[:, a:a + CW], T.MA[:, a:a + CW], T.MB[:, a:a + CW], -256.0, A.add, A.add), ze[c])
 
-    def lower(j):
-        b, a, w, e = parts[j]
-        need("t", cs["ct"])
-        t.matmul(T[b][:, 0:w], T.TRI[:], T.M[:, a:a + w], True, False)
+    def lower(c):
+        need("t", cs["ct"], ze[c])
+        a = CW * c
+        out = T["ps%d" % c][:, 0:4]
+        t.matmul(out, T.TRI[:], T.Z[:, a + KW:a + CW:KW], True, False)
+        done(t.matmul(out, T.NTI[:], T.Z[:, a:a + CW - 1:KW], False, True), pe[c])
 
-    def take(j):
-        b, a, w, e = parts[j]
-        need("t", cs["ci"], scv[min(j, 2)])
-        done(t.matmul(T[b][:, 0:w], T.IDN[:], T.SC[:, a:a + w], False, True), sub[j])
+    def base(c):
+        need("v", pe[c])
+        done(v.tensor_scalar(T.BASE[:, 4 * c:4 * c + 4], T["ps%d" % c][:, 0:4], T.QF[:, 5:6], None, A.add), bs[c])
 
-    def cut(j):
-        b, a, w, e = parts[j]
-        need(e, sub[j])
-        if e == "s":
-            done(s.activation(T.P[:, a:a + w], T[b][:, 0:w], RELU, bias=-LIFT - 1.0), pe[j])
-        else:
-            done(v.tensor_scalar(T.P[:, a:a + w], T[b][:, 0:w], -LIFT - 1.0, 0.0, A.add, A.max), pe[j])
+    def cut(q, c):
+        need(q, bs[c], ze[c])
+        n = share[c]
+        for j in (range(0, n) if q == "v" else range(n, 4)):
+            k = 4 * c + j
+            a = CW * c + KW * j + 1
+            if q == "v":
+                done(v.tensor_scalar(T.P[:, F * k:F * k + F], T.Z[:, a:a + F], T.BASE[:, k:k + 1], 0.0, A.add, A.max), ce[c])
+            else:
+                done(s.activation(T.P[:, F * k:F * k + F], T.Z[:, a:a + F], RELU, bias=T.BASE[:, k:k + 1]), ce[c])
 
-    def add(j, first=False, end=False):
-        b, a, w, e = parts[j]
-        need("t", pe[j])
-        for i in range(a, a + w, F):
-            inst = t.matmul(T.ps7[:, 0:F], T.IDN[:], T.P[:, i:i + F], first and i == a, end and i == a + w - F)
-        if end:
+    def add(c):
+        need("t", cs["cv"], cs["ci"], ce[c])
+        for k in range(4 * c, 4 * c + 4):
+            inst = t.matmul(T.ps7[:, 0:F], lhs, T.P[:, F * k:F * k + F], k == 0 and not kinds, k == N - 1)
+        if c == 2:
             done(inst, last)
 
     masks(0)
-    totals(0)
+    behind(0)
     step(0)
     masks(1)
-    totals(1)
-    lower(0)
-    lower(1)
+    behind(1)
     step(1)
     scan(0)
+    lower(0)
     masks(2)
-    need("t", scv[0])
-    totals(2)
-    lower(2)
-    take(0)
+    behind(2)
     scan(1)
-    take(1)
-    lower(3)
+    lower(1)
     step(2)
-    cut(0)
-    scan(2)
-    take(2)
-    take(3)
+    base(0)
+    cut("s", 0)
     step(3)
-    cut(1)
-    cut(2)
-    cut(3)
-    add(0, True)
+    scan(2)
+    lower(2)
+    base(1)
+    cut("v", 0)
+    cut("s", 1)
+    cut("v", 1)
+    base(2)
+    cut("v", 2)
+    cut("s", 2)
     step(4)
+    add(0)
     add(1)
     add(2)
-    add(3, False, True)
 
 
 def codes_of(g, T, tk, load_s, load_d, extra):
@@ -314,6 +357,63 @@ def codes_of(g, T, tk, load_s, load_d, extra):
     need("v", c)
 
 
+def columns(g, T, tk, cs, win, starts, bank, out, ev):
+    new, done, need, finish = tk
+    e = new()
+    need("t", win, cs["cv"])
+    for i, a in enumerate(starts):
+        inst = g.tensor.matmul(T[bank][:, 16 * i:16 * i + 16], T.WIN[:, a:a + 128], T.REP[:], True, True)
+    done(inst, e)
+    n = 16 * len(starts)
+    need("v", e, cs["cm"])
+    done(g.vector.tensor_tensor(out, T[bank][:, 0:n], T.MK[:, 0:n], A.mult), ev)
+
+
+def addr_of(core, topo, d):
+    rid, pid = topo.addr(d, core)
+    return DstId(rid=rid, pnc=pid)
+
+
+def send_lists(g, core, T, topo, srcs, dests, eng, sem):
+    h = len(eng) // 2
+    trs = []
+    for k in range(2):
+        trs.append(RemoteDMATransfer(dst_ids=[addr_of(core, topo, d[0]) for d in dests], dma_engine_mask=together(eng[h * k:h * k + h]),
+                                     remote_sem=sem, srcs=[srcs[k]], dsts=[d[1 + k] for d in dests]))
+    g.remote_dma_fused(trs, local_sem=T.sem.ls)
+    return len(eng)
+
+
+def send_block(g, core, T, topo, dest, out, in_, sem, eng=None):
+    eng = eng or shared_engines(topo, core, [dest])
+    rid, pid = topo.addr(dest, core)
+    g.remote_dma(out, in_, sem, T.sem.ls, pid, rid, together(eng))
+    return len(eng)
+
+
+def landing(T, h):
+    return T.W[:, R + CAPP * h:R + CAPP * h + CAPP]
+
+
+def relay_list(g, core, T, topo, buf, r):
+    peer = layout(T, topo, r)[0]
+    off = leaving_engines(topo, core)
+    k = slot_of(T, topo, peer)
+    ds = [other_helper_of(T.cores[t], topo) for t in layout(T, topo, peer)[1]]
+    g.wait_ge(T.sem.lp, len(off) // 2)
+    tr = RemoteDMATransfer(dst_ids=[addr_of(core, topo, d) for d in ds], dma_engine_mask=together(off), remote_sem=T.sem.la,
+                           srcs=[buf[k]], dsts=[buf[k] for d in ds])
+    g.remote_dma_fused([tr], local_sem=T.sem.ls)
+    return len(off)
+
+
+def relay_block(g, core, T, topo, r, i):
+    peer = layout(T, topo, r)[0]
+    t = layout(T, topo, peer)[1][i]
+    g.wait_ge(T.sem["di%d" % i], len(leaving_engines(topo, core)))
+    return send_block(g, core, T, topo, T.cores[t], landing(T, peer), T.DG[:, CAPP * i:CAPP * i + CAPP], T.sem.da)
+
+
 def load_lists(g, T, tk, waits):
     new, done, need, finish = tk
     ls, ld = new(), new()
@@ -325,101 +425,76 @@ def load_lists(g, T, tk, waits):
     return ls, ld
 
 
-def list_transfer(core, T, topo, buf, r, dests, eng, sem):
-    ids = []
-    for d in dests:
-        rid, pid = topo.addr(d, core)
-        ids.append(DstId(rid=rid, pnc=pid))
-    return RemoteDMATransfer(dst_ids=ids, dma_engine_mask=together(eng), remote_sem=sem, srcs=[buf[r]], dsts=[buf[r] for d in dests])
+def forwarded(far):
+    return far[2]
 
 
-def send_lists(g, core, T, topo, r, dests, sem, dests_d=None):
-    dd = dests_d or dests
-    eng = shared_engines(topo, core, dd)
-    h = len(eng) // 2
-    g.remote_dma_fused([list_transfer(core, T, topo, T.Ls, r, dests, eng[:h], sem),
-                        list_transfer(core, T, topo, T.Ld, r, dd, eng[h:], sem)], local_sem=T.sem.ls)
-    return len(eng)
+def shares(r, diag, far, mate, same):
+    return [diag[2], forwarded(far), far[1]] + same + [mate[2], r], [diag[0], diag[1], far[0]] + mate[:2]
 
 
-def send_list(g, core, T, topo, buf, r, dests, sem):
-    eng = shared_engines(topo, core, dests)
-    g.remote_dma_fused([list_transfer(core, T, topo, buf, r, dests, eng, sem)], local_sem=T.sem.ls)
-    return len(eng)
+def gathered(T, r, d, i, a, b):
+    if d == r:
+        return T.W[:, R + CAPP * r + a:R + CAPP * r + b]
+    return T.G[:, CAPP * i + a:CAPP * i + b]
 
 
-def send_block(g, core, T, topo, dest, out, in_, sem, inside=False):
-    eng = inside_engines(topo, core, dest) if inside else shared_engines(topo, core, [dest])
-    rid, pid = topo.addr(dest, core)
-    g.remote_dma(out, in_, sem, T.sem.ls, pid, rid, together(eng))
-    return len(eng)
-
-
-def landing(T, h):
-    return T.W[:, R + CAPP * h:R + CAPP * h + CAPP]
-
-
-def gather(g, T, tk, ts):
-    new, done, need, finish = tk
-    v, s = g.vector, g.scalar
-    evs = [new() for t in ts]
-
-    def part(q, j, a, w):
-        b = CAPP * ts[j] + a
-        src = T.W[:, 0:R].indirect(T.GO[:, b // 16:(b + w) // 16])
-        if q == "v":
-            done(v.tensor_copy(T.G[:, b:b + w], src), evs[j])
-        else:
-            done(s.activation(T.G[:, b:b + w], src, COPY), evs[j])
-
-    for j in range(len(ts)):
-        if j % 2 == 0 and j == len(ts) - 1:
-            part("v", j, 0, CAPP // 2)
-            part("s", j, CAPP // 2, CAPP // 2)
-        else:
-            part("vs"[j % 2], j, 0, CAPP)
-    return evs
-
-
-def shares(diag, far, mate, same):
-    return [(diag, far), (mate + same[:1], same[1:])]
-
-
-def source_rank(g, core, T, topo, r):
+def source(g, core, T, topo, r, is_rank):
     tk = tools(g, T)
     new, done, need, finish = tk
-    v, s = g.vector, g.scalar
-    peer, diag, far, mate, same, direct = layout(T, topo, r)
-    sec = second_of(core, topo)
-    left = 0
-    pr = new()
-    done(g.sync.dma_start(T.Ls[r], T.src[:]), pr, 16)
-    done(s.dma_start(T.Ld[r], T.dst[:]), pr, 16)
-    cs = constants(g, T, tk, True)
-    need("g", pr)
+    v, s, t = g.vector, g.scalar, g.tensor
+    peer, diag, far, mate, same = layout(T, topo, r)
+    rank = T.cores[r]
+    sec = second_of(rank, topo)
     pc = T.cores[peer]
-    ph = helper_of(pc, topo)
-    k = send_lists(g, core, T, topo, r, [pc, ph], T.sem.lp, [pc, ph, second_of(pc, topo)])
-    left += k
-    rest = [t for t in direct if t != peer]
-    ds = [T.cores[t] for t in rest] + [helper_of(T.cores[t], topo) for t in rest] + [helper_of(core, topo)]
-    left += send_lists(g, core, T, topo, r, ds, T.sem.la)
-    on = [T.cores[t] for t in layout(T, topo, peer)[1]]
-    g.wait_ge(T.sem.lp, k)
-    left += send_lists(g, core, T, topo, peer, on, T.sem.la)
-    cs["late"]()
-    need("y", pr)
-    need("s", pr)
-    load_s, load_d = load_lists(g, T, tk, [(T.sem.lp, k), (T.sem.la, k * (N - 2))])
+    down = downwards(T, topo, r, is_rank)
+    off = leaving_engines(topo, core)
+    ne = len(off)
+    h = ne // 2
+    left = 0
     tabs = [new(), new()]
-    need("y", load_s, load_d)
-    for j in range(2):
+
+    def load_table(j):
         a = R // 2 * j
         done(g.sync.dma_start(T.W[:, a:a + R // 2], T.tab[:, a:a + R // 2]), tabs[j], 16)
-        need("g", tabs[j])
-        left += send_block(g, core, T, topo, sec, T.W[:, a:a + R // 2], T.W[:, a:a + R // 2], T.sem.tb)
 
-    sl, hi, lo, nm1, nm2 = new(), new(), new(), new(), new()
+    def copy_table(j):
+        a = R // 2 * j
+        need("g", tabs[j])
+        return send_block(g, core, T, topo, sec, T.W[:, a:a + R // 2], T.W[:, a:a + R // 2], T.sem.tb)
+
+    if is_rank:
+        k = slot_of(T, topo, r)
+        pr = new()
+        done(g.sync.dma_start(T.Ls[k], T.src[:]), pr, 16)
+        done(s.dma_start(T.Ld[k], T.dst[:]), pr, 16)
+        cs = constants(g, T, tk, True, down)
+        need("y", pr)
+        load_table(0)
+        need("g", pr)
+        srcs = [T.Ls[k], T.Ld[k]]
+        ds = [second_of(pc, topo), other_helper_of(pc, topo), helper_of(core, topo)]
+        left += send_lists(g, core, T, topo, srcs, [(pc, T.Ps[0], T.Pd[0])] + [(c, T.Ls[k], T.Ld[k]) for c in ds], off[:h], T.sem.lp)
+        rest = [d for d in far if d != peer]
+        ds = [second_of(T.cores[d], topo) for d in rest] + [T.cores[d] for d in mate + same] + [other_helper_of(T.cores[d], topo) for d in rest]
+        left += send_lists(g, core, T, topo, srcs, [(c, T.Ls[k], T.Ld[k]) for c in ds], off[h:], T.sem.la)
+        g.wait_ge(T.sem.lp, h)
+        p = slot_of(T, topo, peer)
+        ds = [second_of(T.cores[d], topo) for d in layout(T, topo, peer)[1]]
+        left += send_lists(g, core, T, topo, [T.Ps[0], T.Pd[0]], [(c, T.Ls[p], T.Ld[p]) for c in ds], off[:h], T.sem.la)
+        cg = cs["late"]()
+        need("s", pr)
+        load_s, load_d = load_lists(g, T, tk, [(T.sem.la, h * (NL - 1))])
+        load_table(1)
+        left += copy_table(0)
+        left += copy_table(1)
+    else:
+        cs = constants(g, T, tk, True, down)
+        cg = cs["late"]()
+        left += relay_list(g, core, T, topo, T.Ls, r)
+        load_s, load_d = load_lists(g, T, tk, [(T.sem.lp, h), (T.sem.la, h * (NL - 1))])
+
+    sl, hi, lo, nm, nk = new(), new(), new(), new(), new()
 
     def take_sl():
         done(v.tensor_scalar(T.SL[:], T.S[:], float(-R * r), None, A.add), sl)
@@ -427,9 +502,14 @@ def source_rank(g, core, T, topo, r):
         done(s.activation(T.HI[:], T.SL[:], COPY), hi)
 
     codes_of(g, T, tk, load_s, load_d, take_sl)
-    vv, ee = new(), new()
-    bank = [T.ps3[:, 0:F], T.ps3[:, F:2 * F]]
-    x, mine, gm = new(), new(), new()
+    vv, ee, x = new(), new(), new()
+    bank = [T.ps3[:, 0:F], T.ps6[:, 0:F]]
+
+    def kinds(c, me):
+        need("t", cs["si"], me)
+        for d in range(max(1, 4 * c), 4 * c + 4):
+            a = CW * c + KW * (d % 4) + 1
+            t.matmul(T.ps7[:, 0:F], T.DI[:, 128 * d:128 * d + 128], T.MA[:, a:a + F], d == 1, False)
 
     def step(c):
         if c == 0:
@@ -437,164 +517,184 @@ def source_rank(g, core, T, topo, r):
             done(v.tensor_tensor(T.LO[:], T.SL[:], T.HI[:], A.subtract), lo)
             need("t", cs["cv"], hi, lo)
             for j in range(2):
-                done(g.tensor.matmul(bank[j], T.PRM[:, 256 * j:256 * j + 128], T.HI[:], True, False), ee)
-                done(g.tensor.matmul(bank[j], T.PRM[:, 256 * j + 128:256 * j + 256], T.LO[:], False, True), ee)
-            need("s", cs["cv"], ee)
-            spread(("s", s), T, tk, vv, range(0, 10), bank)
+                done(t.matmul(bank[j], T.PRM[:, 256 * j:256 * j + 128], T.HI[:], True, False), ee)
+                done(t.matmul(bank[j], T.PRM[:, 256 * j + 128:256 * j + 256], T.LO[:], False, True), ee)
         if c == 1:
-            done(v.tensor_scalar(T.MN[:, 0:F], T.HS[:], float(16 * r), None, A.is_equal), mine)
-            done(v.tensor_scalar(T.MN[:, F:2 * F], T.HS[:], float(16 * r), None, A.not_equal), nm1)
+            need("s", cs["cv"], ee)
+            spread(("s", s), T, tk, vv, range(0, 6, 2), bank)
         if c == 2:
-            need("v", mine, nm1, cs["cg"])
-            done(v.tensor_tensor(T.MN[:, 2 * F:3 * F], T.MN[:, 0:F], T.GD[:], A.mult), gm)
+            done(v.tensor_scalar(T.NM[:], T.HS[:], float(16 * r), None, A.not_equal), nm)
+            spread(("s", s), T, tk, vv, range(6, 12, 2), bank)
         if c == 3:
-            done(v.tensor_tensor(T.MN[:, 3 * F:4 * F], T.MN[:, F:2 * F], T.K16[:, 0:F], A.mult), nm2)
-            spread(("s", s), T, tk, vv, range(10, 16), bank)
+            need("v", nm, cg)
+            done(v.tensor_tensor(T.NK[:], T.NM[:], T.K16[:], A.mult), nk)
         if c == 4:
-            need("t", cs["si"], nm1, gm, nm2)
-            g.tensor.matmul(T.ps7[:, 0:F], T.SI[:, 0:128], T.MN[:, 2 * F:3 * F], False, False)
-            g.tensor.matmul(T.ps7[:, 0:F], T.SI[:, 128:256], T.MN[:, F:2 * F], False, False)
-            g.tensor.matmul(T.ps7[:, 0:F], T.IDN[:], T.MN[:, 3 * F:4 * F], False, False)
+            spread(("s", s), T, tk, vv, [12, 14] + list(range(1, 16, 2)), bank)
+            need("t", nm, nk)
+            t.matmul(T.ps7[:, 0:F], T.DQ[:], T.NM[:], False, False)
+            t.matmul(T.ps7[:, 0:F], T.IDN[:], T.NK[:], False, False)
 
-    numbers(g, T, tk, cs, [16 * r + t for t in range(N)], step, x)
+    numbers(g, T, tk, cs, [16 * r + d for d in range(N)], T.NID[:] if down else T.IDN[:], (3, 3, 3), step, x, kinds)
     o = new()
     need("v", x)
-    done(v.tensor_scalar(T.O[:], T.ps7[:, 0:F], float(TR), None, A.add), o)
+    done(v.tensor_scalar(T.O[:], T.ps7[:, 0:F], float(TR + 255 if down else TR), None, A.add), o)
     need("v", o, vv)
     win = new()
-    done(v.tensor_copy(T.WIN[:, 0:TR + LAND].indirect(T.O[:, 0:F]), T.V[:]), win)
-    need("t", win)
-    parts = shares(diag, far, mate, same)
-    first = [min(parts[0][0] + parts[0][1]), min(parts[1][0] + parts[1][1] + [r])]
-    wr, go = [new(), new()], [new(), new()]
-    for c in range(2):
-        st = TR + CAPP * first[c]
-        for j in range(16):
-            inst = g.tensor.matmul(T["ps%d" % (1 + c)][:, 0:F], sel(T, j), T.WIN[:, st + j:st + 16 * F:16], j == 0, j == 15)
-        done(inst, wr[c])
-    n = 0
-    for c in range(2):
-        ours, hers = parts[c]
-        a = 16 * first[c]
-        need("v", wr[c])
-        done(v.tensor_copy(T.GO[:, a:a + F], T["ps%d" % (1 + c)][:, 0:F]), go[c])
-        need("g", go[c])
-        b, w = 16 * min(hers), 16 * len(hers)
-        left += send_block(g, core, T, topo, sec, T.GO[:, b:b + w], T.GO[:, b:b + w], T.sem["g%d" % c], True)
-        need("v", go[c], *tabs)
-        need("s", go[c], *tabs)
-        evs = gather(g, T, tk, ours)
-        for i, t in enumerate(ours):
-            need("g", evs[i])
-            blk = T.G[:, CAPP * t:CAPP * t + CAPP]
-            if c == 0:
-                n = send_block(g, core, T, topo, ph, T.DG[:, CAPP * i:CAPP * i + CAPP], blk, T.sem["di%d" % i])
+    done(v.tensor_copy(T.WIN[:, 0:TR + LAND].indirect(T.O[:]), T.V[:]), win)
+    ours, hers = shares(r, diag, far, mate, same)
+    if not is_rank:
+        ours, hers = hers, ours
+    rx, ro, ge, go = [[new(), new()] for _ in range(4)]
+
+    def halfway(ts, out, banks, ev):
+        for c, (a, b) in enumerate(PARTS):
+            starts = [TR + CAPP * d + u for d in ts[a:b] for u in (0, 128)]
+            columns(g, T, tk, cs, win, starts, banks[c], out[:, BC * a:BC * min(b, len(ts))], ev[c])
+
+    halfway(hers, T.RX, ("ps4", "ps5"), rx)
+    halfway(ours, T.RO, ("ps1", "ps2"), ro)
+    for c, (a, b) in enumerate(PARTS):
+        need("g", rx[c])
+        b = min(b, len(hers))
+        left += send_block(g, core, T, topo, sec if is_rank else rank, T.RI[:, BC * a:BC * b], T.RX[:, BC * a:BC * b], T.sem["xs%d" % c], off)
+    if is_rank:
+        need("v", *tabs)
+        need("s", *tabs)
+    else:
+        for q in (v, s):
+            q.wait_ge(T.sem.tb, 2 * len(shared_engines(topo, rank, [core])))
+    for c, (a, b) in enumerate(PARTS):
+        b = min(b, len(ours))
+        out = T[("ps0", "ps6")[c]][:, 0:16 * (b - a)]
+        need("t", ro[c], cs["cm"])
+        t.matmul(out, T.L16[:], T.RO[:, BC * a:BC * b:2], True, False)
+        t.matmul(out, T.L16[:], T.RO[:, BC * a + 1:BC * b:2], False, False)
+        t.wait_ge(T.sem["xs%d" % c], ne)
+        t.matmul(out, T.L16[:], T.RI[:, BC * a:BC * b:2], False, False)
+        done(t.matmul(out, T.L16[:], T.RI[:, BC * a + 1:BC * b:2], False, True), ge[c])
+        need("v", ge[c])
+        done(v.tensor_copy(T.GO[:, 16 * a:16 * b], out), go[c])
+        need("v", go[c])
+        need("s", go[c])
+        for i in range(a, b):
+            d = ours[i]
+            e = new()
+            cols = [("vs"[(i - a) % 2], 0, CAPP)]
+            if i == b - 1 and (b - a) % 2:
+                cols = [("v", 0, CAPP // 2), ("s", CAPP // 2, CAPP)]
+            for q, x0, x1 in cols:
+                src = T.W[:, 0:R].indirect(T.GO[:, 16 * i + x0 // 16:16 * i + x1 // 16])
+                if q == "v":
+                    done(v.tensor_copy(gathered(T, r, d, i, x0, x1), src), e)
+                else:
+                    done(s.activation(gathered(T, r, d, i, x0, x1), src, COPY), e)
+            if d == r:
+                own = e
+                continue
+            need("g", e)
+            blk = gathered(T, r, d, i, 0, CAPP)
+            if d in diag:
+                j = diag.index(d)
+                to = diag_sender(j, helper_of(pc, topo), other_helper_of(pc, topo))
+                left += send_block(g, core, T, topo, to, T.DG[:, CAPP * j:CAPP * j + CAPP], blk, T.sem["di%d" % j])
+            elif d == forwarded(far):
+                to = helper_of(rank, topo)
+                inside = [b_ for b_ in shared_engines(topo, core, [to]) if b_ not in off]
+                left += send_block(g, core, T, topo, to, T.FW[:], blk, T.sem.fw, inside)
             else:
-                n = send_block(g, core, T, topo, T.cores[t], landing(T, r), blk, T.sem.da)
-            left += n
-    own = new()
-    done(v.tensor_copy(landing(T, r), T.W[:, 0:R].indirect(T.GO[:, 16 * r:16 * r + 16])), own)
-    inv = len(inside_engines(topo, helper_of(core, topo), core))
-    for q in (v, s):
-        q.wait_ge(T.sem.iv, inv)
-        q.wait_ge(T.sem.da, n * (N - 1))
-    need("v", own)
-    need("s", own)
-    at = 0
-    yo = new()
-    for j, w in enumerate((512, 512, 768, 768, 768, 768)):
-        src = T.W[:].indirect(T.INV[:, at // 16:(at + w) // 16])
-        e = new()
-        if j % 2 == 0:
-            done(v.tensor_copy(T.Y[:, at:at + w], src), e)
-        else:
-            done(s.activation(T.Y[:, at:at + w], src, COPY), e)
-        need("y", e)
-        done(g.sync.dma_start(T.y[:, at:at + w], T.Y[:, at:at + w]), yo, 16)
-        at += w
-    need("y", yo)
+                left += send_block(g, core, T, topo, T.cores[d], landing(T, r), blk, T.sem.da)
+    if is_rank:
+        cg2, tc, inv, ej, y0 = new(), new(), new(), new(), new()
+        done(g.iota(T.TC[:], [[16, R // 16]], 0, 0, allow_small_or_imprecise_dtypes=True), cg2)
+        need("v", cg2)
+        done(v.tensor_scalar(T.TC[:], T.TC[:], T.QF[:, 0:1], None, A.add), tc)
+        t.wait_ge(T.sem.iv, 2 * ne)
+        out = T.ps7[:, 0:R // 16]
+        t.matmul(out, T.L16[:], T.RA[:, 0:512:2], True, False)
+        t.matmul(out, T.L16[:], T.RA[:, 1:512:2], False, False)
+        t.matmul(out, T.L16[:], T.RB[:, 0:512:2], False, False)
+        done(t.matmul(out, T.L16[:], T.RB[:, 1:512:2], False, True), y0)
+        need("v", y0, tc)
+        done(v.tensor_tensor(T.EE[:], T.TC[:], out, A.max), ej)
+        need("v", ej)
+        done(v.tensor_copy(T.INV[:], T.EE[:]), inv)
+        for q in (v, s):
+            q.wait_ge(T.sem.da, ne * (N - 1))
+        need("v", inv, own)
+        need("s", inv, own)
+        at = 0
+        yo = new()
+        for j, w in enumerate((640, 640, 768, 768, 640, 640)):
+            src = T.W[:].indirect(T.INV[:, at // 16:(at + w) // 16])
+            e = new()
+            if j % 2 == 0:
+                done(v.tensor_copy(T.Y[:, at:at + w], src), e)
+            else:
+                done(s.activation(T.Y[:, at:at + w], src, COPY), e)
+            need("y", e)
+            done(g.sync.dma_start(T.y[:, at:at + w], T.Y[:, at:at + w]), yo, 16)
+            at += w
+        need("y", yo)
     g.wait_ge(T.sem.ls, left)
     finish()
 
 
-def second(g, core, T, topo, r):
+def helper(g, core, T, topo, r, own):
     tk = tools(g, T)
     new, done, need, finish = tk
-    peer, diag, far, mate, same, direct = layout(T, topo, r)
-    on = [helper_of(T.cores[t], topo) for t in layout(T, topo, peer)[1]]
-    g.wait_ge(T.sem.lp, len(shared_engines(topo, T.cores[peer], [core])) // 2)
-    left = send_list(g, core, T, topo, T.Ld, peer, on, T.sem.la)
-    rank = T.cores[r]
-    tab = 2 * len(shared_engines(topo, rank, [core]))
-    for c, (ours, hers) in enumerate(shares(diag, far, mate, same)):
-        for q in (g.vector, g.scalar):
-            if c == 0:
-                q.wait_ge(T.sem.tb, tab)
-            q.wait_ge(T.sem["g%d" % c], len(inside_engines(topo, rank, core)))
-        evs = gather(g, T, tk, hers)
-        for i, t in enumerate(hers):
-            need("g", evs[i])
-            left += send_block(g, core, T, topo, T.cores[t], landing(T, r), T.G[:, CAPP * t:CAPP * t + CAPP], T.sem.da)
-    g.wait_ge(T.sem.ls, left)
-    finish()
-
-
-def helper(g, core, T, topo, r):
-    tk = tools(g, T)
-    new, done, need, finish = tk
-    v, s = g.vector, g.scalar
-    peer, diag, far, mate, same, direct = layout(T, topo, r)
+    v, s, t = g.vector, g.scalar, g.tensor
+    peer, diag, far, mate, same = layout(T, topo, r)
+    down = downwards(T, topo, r, own)
+    off = leaving_engines(topo, core)
+    ne = len(off)
     left = 0
-    cs = constants(g, T, tk, False)
-    cs["late"]()
-    td, tc = [new(), new()], new()
-    need("v", cs["cg"], cs["q"])
-    done(v.tensor_scalar(T.TD[:, 0:F], T.K16[:, 0:F], T.QF[:, 0:1], float(R), A.add, A.add), td[0])
-    done(v.tensor_scalar(T.TC[:], T.K16[:], T.QF[:, 0:1], None, A.add), tc)
+    cs = constants(g, T, tk, False, down)
+    cg = cs["late"]()
+    td = [new(), new()]
+    mine, place = T.U[:, 3 * F:4 * F], T.U[:, 4 * F:5 * F]
+    need("v", cg, cs["q"])
+    done(v.tensor_scalar(place, T.K16[:], T.QF[:, 0:1], None, A.add), td[0])
     need("v", td[0])
-    done(v.tensor_scalar(T.TD[:, F:2 * F], T.TD[:, 0:F], float(R * r), None, A.add), td[1])
-    on = layout(T, topo, peer)[1]
-    ne = len(shared_engines(topo, core, [T.cores[t] for t in on]))
-    g.wait_ge(T.sem.lp, ne)
-    left += send_list(g, core, T, topo, T.Ls, peer, [helper_of(T.cores[t], topo) for t in on], T.sem.la)
-    load_s, load_d = load_lists(g, T, tk, [(T.sem.lp, ne), (T.sem.la, ne * (N - 1) + ne * len(diag))])
-
-    def pass_on(i):
-        g.wait_ge(T.sem["di%d" % i], ne)
-        return send_block(g, core, T, topo, T.cores[on[i]], landing(T, peer), T.DG[:, CAPP * i:CAPP * i + CAPP], T.sem.da)
-
-    left += pass_on(0)
-    left += pass_on(1)
-
+    done(v.tensor_scalar(T.U[:, 5 * F:6 * F], place, float(R * r), None, A.add), td[1])
+    if own:
+        g.wait_ge(T.sem.lp, ne // 2)
+        k = slot_of(T, topo, r)
+        ds = [(helper_of(T.cores[d], topo), T.Ls[k], T.Ld[k]) for d in mate + same]
+        left += send_lists(g, core, T, topo, [T.Ls[k], T.Ld[k]], ds, off, T.sem.la)
+        waits = [(T.sem.lp, ne // 2), (T.sem.la, ne * (NL - 1))]
+    else:
+        left += relay_list(g, core, T, topo, T.Ld, r)
+        waits = [(T.sem.lp, ne // 2), (T.sem.la, ne // 2 * 2 + ne * 6)]
+    load_s, load_d = load_lists(g, T, tk, waits)
     codes_of(g, T, tk, load_s, load_d, lambda: None)
-    a, h0, hi, b, c, o, oo = new(), new(), new(), new(), new(), new(), new()
+    a, hi, b, c, o, oo = new(), new(), new(), new(), new(), new()
     x, lo, ee, vv = new(), new(), [new(), new()], new()
-    bank = [T.ps3[:, 0:F], T.ps2[:, 0:F]]
+    bank = [T.ps3[:, 0:F], T.ps6[:, 0:F]]
 
     def step(ch):
-        if ch == 0:
-            done(v.tensor_scalar(T.MM[:], T.GD[:], float(r), None, A.is_equal), a)
-            done(v.tensor_scalar(T.SL[:], T.HS[:], float(CAPP // 16), float(R), A.mult, A.add), h0)
-        if ch == 1:
-            need("v", a, h0)
-            done(v.tensor_tensor(T.HI[:], T.SL[:], T.MM[:], A.mult), hi)
         if ch == 2:
-            need("v", *td)
-            done(v.tensor_tensor(T.U[:, 0:F], T.D[:], T.TD[:, F:2 * F], A.subtract), b)
+            done(v.tensor_scalar(T.HI[:], T.HS[:], float(CAPP // 16), float(R), A.mult, A.add), hi)
+            need("t", cs["cv"], hi)
+            for j in range(2):
+                t.matmul(bank[j], T.PRM[:, 256 * j:256 * j + 128], T.HI[:], True, False)
+        if ch == 3:
+            done(v.tensor_scalar(mine, T.GD[:], float(r), None, A.is_equal), a)
+            need("v", td[1])
+            done(v.tensor_tensor(T.U[:, 0:F], T.D[:], T.U[:, 5 * F:6 * F], A.subtract), b)
 
-    numbers(g, T, tk, cs, [16 * h + r for h in range(N)], step, x)
+    numbers(g, T, tk, cs, [16 * d + r for d in range(N)], T.IDN[:], (1, 2, 2), step, x, None)
     need("s", x)
-    done(s.activation(T.LO[:], T.ps7[:, 0:F], COPY), lo)
-    need("t", cs["cv"], hi)
-    for j in range(2):
-        g.tensor.matmul(bank[j], T.PRM[:, 256 * j:256 * j + 128], T.HI[:], True, False)
+    if down:
+        done(s.activation(T.LO[:], T.ps7[:, 0:F], RELU, bias=255.0, scale=-1.0), lo)
+    else:
+        done(s.activation(T.LO[:], T.ps7[:, 0:F], COPY), lo)
     need("t", lo)
     for j in range(2):
-        done(g.tensor.matmul(bank[j], T.PRM[:, 256 * j + 128:256 * j + 256], T.LO[:], False, True), ee[j])
+        done(t.matmul(bank[j], T.PRM[:, 256 * j + 128:256 * j + 256], T.LO[:], False, True), ee[j])
     need("v", a, b)
-    done(v.tensor_tensor(T.U[:, F:2 * F], T.U[:, 0:F], T.MM[:], A.mult), c)
+    done(v.tensor_tensor(T.U[:, F:2 * F], T.U[:, 0:F], mine, A.mult), c)
     need("v", c)
-    done(v.tensor_tensor(T.U[:, 2 * F:3 * F], T.U[:, F:2 * F], T.TD[:, 0:F], A.add), o)
+    done(v.tensor_tensor(T.U[:, 2 * F:3 * F], T.U[:, F:2 * F], place, A.add), o)
     need("v", o)
     done(v.tensor_copy(T.O[:], T.U[:, 2 * F:3 * F]), oo)
     need("s", cs["cv"], ee[0])
@@ -603,24 +703,19 @@ def helper(g, core, T, topo, r):
     spread(("v", v), T, tk, vv, range(1, 16, 2), bank)
     need("v", oo, vv)
     win = new()
-    done(v.tensor_copy(T.WIN[:, 0:R + TR].indirect(T.O[:, 0:F]), T.V[:]), win)
-    need("t", win)
-    n = R // 32
-    d = new()
-    for half in range(2):
-        pw, ej = new(), new()
-        ps = T["ps%d" % (4 + half)][:, 0:n]
-        for j in range(16):
-            inst = g.tensor.matmul(ps, sel(T, j), T.WIN[:, R // 2 * half + j:R // 2 * (half + 1):16], j == 0, j == 15)
-        done(inst, pw)
-        at = n * half
-        need("v", pw, tc)
-        done(v.tensor_tensor(T.EE[:, at:at + n], T.TC[:, at:at + n], ps, A.max), ej)
-        need("v", ej)
-        done(v.tensor_copy(T.INV[:, at:at + n], T.EE[:, at:at + n]), d)
-    need("g", d)
-    left += send_block(g, core, T, topo, T.cores[r], T.INV[:], T.INV[:], T.sem.iv, True)
-    left += pass_on(2)
+    done(v.tensor_copy(T.WIN[:, 0:R + TR].indirect(T.O[:]), T.V[:]), win)
+    rh = new()
+    for k in range(4):
+        starts = range(1024 * k, 1024 * k + 1024, 128)
+        columns(g, T, tk, cs, win, starts, ("ps4", "ps5", "ps0", "ps1")[k], T.RH[:, 128 * k:128 * k + 128], rh)
+    need("g", rh)
+    left += send_block(g, core, T, topo, T.cores[r], T.RA[:] if own else T.RB[:], T.RH[:], T.sem.iv, off)
+    for i in (0, 2, 1):
+        if diag_sender(i, True, False) == own:
+            left += relay_block(g, core, T, topo, r, i)
+    if own:
+        g.wait_ge(T.sem.fw, ne)
+        left += send_block(g, core, T, topo, T.cores[forwarded(far)], landing(T, r), T.FW[:], T.sem.da)
     g.wait_ge(T.sem.ls, left)
     finish()
 
@@ -629,11 +724,14 @@ def rank_program(g, core, T, topo):
     for r in range(N):
         c = T.cores[r]
         if core == c:
-            source_rank(g, core, T, topo, r)
-            return
-        if core == helper_of(c, topo):
-            helper(g, core, T, topo, r)
+            source(g, core, T, topo, r, True)
             return
         if core == second_of(c, topo):
-            second(g, core, T, topo, r)
+            source(g, core, T, topo, r, False)
+            return
+        if core == helper_of(c, topo):
+            helper(g, core, T, topo, r, True)
+            return
+        if core == other_helper_of(c, topo):
+            helper(g, core, T, topo, r, False)
             return

from concourse.bass import DstId, RemoteDMATransfer
from concourse.mybir import AluOpType, ActivationFunctionType

N = 12
CAPP = 256
R = 4096
L = 1024
NL = N // 2
F = NL * L // 128
KW = F + 1
CW = 4 * KW + 1
LAND = N * CAPP
TR = 16 * F
BC = CAPP // 8
NB = 7
PARTS = [(0, 3), (3, NB)]
COPY = ActivationFunctionType.Copy
RELU = ActivationFunctionType.Relu
A = AluOpType

SCRATCH = {
    "Ls": ("dram", [NL, 128, L // 128], "int32"),
    "Ld": ("dram", [NL, 128, L // 128], "int32"),
    "Ps": ("dram", [1, 128, L // 128], "int32"),
    "Pd": ("dram", [1, 128, L // 128], "int32"),
    "S": ("sbuf", [128, F], "int32"),
    "D": ("sbuf", [128, F], "int32"),
    "HS": ("sbuf", [128, F], "int32"),
    "GD": ("sbuf", [128, F], "int32"),
    "CODE": ("sbuf", [128, F], "bfloat16"),
    "MA": ("sbuf", [128, 3 * CW], "bfloat16"),
    "MB": ("sbuf", [128, 3 * CW], "bfloat16"),
    "Z": ("sbuf", [128, 3 * CW], "bfloat16"),
    "P": ("sbuf", [128, N * F], "bfloat16"),
    "BASE": ("sbuf", [128, N], "float32"),
    "SL": ("sbuf", [128, F], "float32"),
    "HI": ("sbuf", [128, F], "bfloat16"),
    "LO": ("sbuf", [128, F], "bfloat16"),
    "V": ("sbuf", [128, TR], "bfloat16"),
    "NM": ("sbuf", [128, F], "bfloat16"),
    "NK": ("sbuf", [128, F], "bfloat16"),
    "O": ("sbuf", [128, F], "uint16"),
    "WIN": ("sbuf", [128, R + TR], "bfloat16"),
    "RO": ("sbuf", [128, NB * BC], "bfloat16"),
    "RX": ("sbuf", [128, NB * BC], "bfloat16"),
    "RI": ("sbuf", [128, NB * BC], "bfloat16"),
    "RH": ("sbuf", [128, 512], "bfloat16"),
    "RA": ("sbuf", [128, 512], "bfloat16"),
    "RB": ("sbuf", [128, 512], "bfloat16"),
    "GO": ("sbuf", [128, NB * 16], "uint16"),
    "INV": ("sbuf", [128, R // 16], "uint16"),
    "G": ("sbuf", [128, NB * CAPP], "bfloat16"),
    "DG": ("sbuf", [128, 3 * CAPP], "bfloat16"),
    "FW": ("sbuf", [128, CAPP], "bfloat16"),
    "W": ("sbuf", [128, R + LAND], "bfloat16"),
    "Y": ("sbuf", [128, R], "bfloat16"),
    "ONE": ("sbuf", [128, 128], "bfloat16"),
    "NEG": ("sbuf", [128, 128], "bfloat16"),
    "IDN": ("sbuf", [128, 128], "bfloat16"),
    "NID": ("sbuf", [128, 128], "bfloat16"),
    "TRI": ("sbuf", [128, 128], "bfloat16"),
    "NTI": ("sbuf", [128, 128], "bfloat16"),
    "DI": ("sbuf", [128, N * 128], "bfloat16"),
    "DQ": ("sbuf", [128, 128], "bfloat16"),
    "PRM": ("sbuf", [128, 4 * 128], "bfloat16"),
    "L16": ("sbuf", [128, 128], "bfloat16"),
    "MK": ("sbuf", [128, 128], "bfloat16"),
    "REP": ("sbuf", [128, 16], "bfloat16"),
    "PI": ("sbuf", [128, 1], "int32"),
    "QI": ("sbuf", [128, 4], "int32"),
    "QF": ("sbuf", [128, 14], "float32"),
    "ROWS": ("sbuf", [128, 280], "float32"),
    "K16": ("sbuf", [128, F], "float32"),
    "TC": ("sbuf", [128, R // 16], "float32"),
    "EE": ("sbuf", [128, R // 16], "float32"),
    "U": ("sbuf", [128, 6 * F], "float32"),
}
for _k in range(8):
    SCRATCH["ps%d" % _k] = ("psum", [128, 512], "float32")
SEMAPHORES = ["lp", "la", "di0", "di1", "di2", "da", "iv", "ls", "tb", "fw", "xs0", "xs1"] + ["e%d" % _k for _k in range(100)]


def bits(mask):
    return [b for b in range(mask.bit_length()) if (mask >> b) & 1]


def together(bs):
    return sum(1 << b for b in bs)


def shared_engines(topo, core, dests):
    m = topo.mask(core, dests[0])
    for d in dests[1:]:
        m = m & topo.mask(core, d)
    return bits(m)


def other_chip(topo, core):
    for d in range(core % 8, core + 1024, 8):
        if topo.same_plane(core, d):
            return d
    return core


def leaving_engines(topo, core):
    return shared_engines(topo, core, [other_chip(topo, core)])


def chip_cores(c, topo, same_die):
    return [x for x in range(max(0, c - 7), c + 8)
            if x != c and topo.host(x) == topo.host(c) and topo.chip(x) == topo.chip(c) and (topo.die(x) == topo.die(c)) == same_die]


def helper_of(c, topo):
    return chip_cores(c, topo, True)[0]


def second_of(c, topo):
    return chip_cores(c, topo, False)[0]


def other_helper_of(c, topo):
    return chip_cores(c, topo, False)[-1]


def rack_of(T, topo, r):
    return topo.rack(topo.host(T.cores[r]))


def slot_of(T, topo, r):
    return [t for t in range(N) if rack_of(T, topo, t) == rack_of(T, topo, r)].index(r)


def downwards(T, topo, r, own):
    return (rack_of(T, topo, r) == rack_of(T, topo, 0)) != own


def layout(T, topo, r):
    c = T.cores[r]
    others = [t for t in range(N) if t != r]
    direct = [t for t in others if topo.may_write(c, T.cores[t])]
    diag = [t for t in others if t not in direct]
    far = [t for t in direct if rack_of(T, topo, t) != rack_of(T, topo, r)]
    peer = [t for t in far if topo.chip(T.cores[t]) == topo.chip(c)][0]
    near = [t for t in direct if t not in far]
    turn = r % 3
    diag = diag[turn:] + diag[:turn]
    far = far[turn:] + far[:turn]
    mate = [t for t in near if topo.host(T.cores[t]) != topo.host(c)]
    mate = mate[turn:] + mate[:turn]
    same = [t for t in near if topo.host(T.cores[t]) == topo.host(c)]
    return peer, diag, far, mate, same


def diag_sender(i, first, second):
    return first if i == 0 else second


def tools(g, T):
    st = {"n": 0}
    q = {"g": g, "v": g.vector, "s": g.scalar, "t": g.tensor, "y": g.sync}
    allev = []

    def new():
        k = st["n"]
        st["n"] = k + 1
        e = {"sem": T.sem["e%d" % k], "t": 0, "w": []}
        allev.append(e)
        return e

    def done(inst, e, n=1):
        inst.then_inc(e["sem"], n)
        e["t"] = e["t"] + n

    def need(name, *evs):
        for e in evs:
            if name not in e["w"]:
                q[name].wait_ge(e["sem"], e["t"])
                e["w"].append(name)

    def finish():
        for e in allev:
            if e["t"] and not e["w"]:
                need("g", e)

    return new, done, need, finish


def constants(g, T, tk, source, down):
    new, done, need, finish = tk
    v, s = g.vector, g.scalar
    one, z, ci, cv, ct, cm = new(), new(), new(), new(), new(), new()
    done(v.memset(T.ONE[:], 1.0), one)
    done(v.memset(T.NEG[:], -1.0), one)
    done(v.memset(T.PRM[:], 0.0), z)
    done(v.memset(T.ROWS[:, 0:16], 0.0), z)
    done(g.iota(T.PI[:], [[1, 1]], 0, 1), ci)
    done(g.iota(T.ROWS[:, 16:24], [[1, 8]], 0, 0, allow_small_or_imprecise_dtypes=True), ci)
    need("g", one)
    done(g.affine_select(T.IDN[:], T.ONE[:], [[-1, 128]], A.is_equal, 0.0, 0, 1), ci)
    for c in range(3):
        done(v.memset(T.MA[:, CW * c:CW * c + CW:KW], 256.0), cv)
    done(v.memset(T.MB[:, 0:3 * CW:CW], 0.0), cv)
    need("v", z)
    e0, e1, q = new(), new(), new()
    done(v.memset(T.ROWS[:, 1:16:2], 1.0), e0)
    need("v", ci)
    done(v.tensor_scalar(T.QI[:, 0:1], T.PI[:], 15, None, A.bitwise_and), e1)
    done(v.tensor_scalar(T.QI[:, 2:3], T.PI[:], 4, None, A.arith_shift_right), e1)
    done(v.tensor_scalar(T.QI[:, 3:4], T.PI[:], 1, None, A.bitwise_and), e1)
    done(v.tensor_scalar(T.QI[:, 1:2], T.PI[:], 1, 7, A.arith_shift_right, A.bitwise_and), e1)
    done(v.tensor_scalar(T.QF[:, 5:6], T.PI[:], -1.0, -1.0, A.mult, A.add), cv)
    need("v", e1)
    done(v.tensor_copy(T.QF[:, 0:4], T.QI[:]), q)
    done(v.tensor_copy(T.PRM[:, 0:128:2], T.IDN[:, 0:128:2]), cv)
    done(v.tensor_copy(T.PRM[:, 129:256:2], T.IDN[:, 0:128:2]), cv)
    done(v.tensor_copy(T.PRM[:, 257:384:2], T.IDN[:, 1:128:2]), cv)
    done(v.tensor_copy(T.PRM[:, 384:512:2], T.IDN[:, 1:128:2]), cv)
    need("v", e0, q)
    done(v.tensor_scalar(T.QF[:, 6:14], T.ROWS[:, 16:24], T.QF[:, 1:2], None, A.is_equal), cv)
    done(v.tensor_scalar(T.REP[:], T.ROWS[:, 0:16], T.QF[:, 3:4], None, A.is_equal), cv)
    si = new()
    if source:
        if down:
            done(v.tensor_scalar(T.NID[:], T.IDN[:], -1.0, None, A.mult), cv)
        qt = new()
        done(v.tensor_scalar(T.QF[:, 4:5], T.QF[:, 0:1], -255.0 if down else 0.0, None, A.add), qt)
        need("s", ci, qt)
        done(s.activation(T.DQ[:], T.IDN[:], COPY, scale=T.QF[:, 4:5]), si)
        for t in range(1, N):
            done(s.activation(T.DI[:, 128 * t:128 * t + 128], T.IDN[:], COPY, scale=float(t)), si)
        done(v.memset(T.WIN[:, TR:TR + LAND], 0.0), cv)
    else:
        done(v.memset(T.WIN[:, 0:R], 0.0), cv)

    def late():
        cg, r16 = new(), new()
        done(g.affine_select(T.TRI[:], T.ONE[:], [[1, 128]], A.is_gt, 0.0, 0, -1), ct)
        done(g.affine_select(T.NTI[:], T.NEG[:], [[1, 128]], A.is_ge, 0.0, 0, -1), ct)
        done(g.iota(T.K16[:], [[16, F]], -TR if source else R, 0, allow_small_or_imprecise_dtypes=True), cg)
        if source:
            done(g.iota(T.ROWS[:, 24:152], [[0, 8], [1, 16]], 0, 0, allow_small_or_imprecise_dtypes=True), r16)
        done(g.iota(T.ROWS[:, 152:280], [[0, 8], [1, 8], [0, 2]], 0, 0, allow_small_or_imprecise_dtypes=True), r16)
        need("v", r16)
        if source:
            done(v.tensor_scalar(T.L16[:], T.ROWS[:, 24:152], T.QF[:, 0:1], None, A.is_equal), cm)
        done(v.tensor_scalar(T.MK[:], T.ROWS[:, 152:280], T.QF[:, 2:3], None, A.is_equal), cm)
        return cg

    return {"ci": ci, "ct": ct, "cv": cv, "cm": cm, "si": si, "q": q, "late": late}


def spread(q, T, tk, ev, ks, bank):
    new, done, need, finish = tk
    for j in ks:
        out, in_, c8 = T.V[:, j:TR:16], bank[j % 2], T.QF[:, 6 + j // 2:7 + j // 2]
        if q[0] == "s":
            done(q[1].activation(out, in_, COPY, scale=c8), ev)
        else:
            done(q[1].tensor_scalar(out, in_, c8, None, A.mult), ev)


def numbers(g, T, tk, cs, codes, lhs, share, step, last, kinds):
    new, done, need, finish = tk
    v, s, t = g.vector, g.scalar, g.tensor
    me, be, ze, pe, bs, ce = [[new() for _ in range(3)] for _ in range(6)]

    def masks(c):
        for j in range(4):
            a = CW * c + KW * j + 1
            done(v.tensor_scalar(T.MA[:, a:a + F], T.CODE[:], float(codes[4 * c + j]), 256.0, A.is_equal, A.mult), me[c])

    def behind(c):
        need("s", cs["cv"], me[c])
        a = CW * c
        done(s.activation(T.MB[:, a + 1:a + CW], T.MA[:, a:a + CW - 1], COPY, scale=-255.0 / 256.0), be[c])
        if kinds:
            kinds(c, me[c])

    def scan(c):
        need("v", cs["cv"], me[c], be[c])
        a = CW * c
        done(v.tensor_tensor_scan(T.Z[:, a:a + CW], T.MA[:, a:a + CW], T.MB[:, a:a + CW], -256.0, A.add, A.add), ze[c])

    def lower(c):
        need("t", cs["ct"], ze[c])
        a = CW * c
        out = T["ps%d" % c][:, 0:4]
        t.matmul(out, T.TRI[:], T.Z[:, a + KW:a + CW:KW], True, False)
        done(t.matmul(out, T.NTI[:], T.Z[:, a:a + CW - 1:KW], False, True), pe[c])

    def base(c):
        need("v", pe[c])
        done(v.tensor_scalar(T.BASE[:, 4 * c:4 * c + 4], T["ps%d" % c][:, 0:4], T.QF[:, 5:6], None, A.add), bs[c])

    def cut(q, c):
        need(q, bs[c], ze[c])
        n = share[c]
        for j in (range(0, n) if q == "v" else range(n, 4)):
            k = 4 * c + j
            a = CW * c + KW * j + 1
            if q == "v":
                done(v.tensor_scalar(T.P[:, F * k:F * k + F], T.Z[:, a:a + F], T.BASE[:, k:k + 1], 0.0, A.add, A.max), ce[c])
            else:
                done(s.activation(T.P[:, F * k:F * k + F], T.Z[:, a:a + F], RELU, bias=T.BASE[:, k:k + 1]), ce[c])

    def add(c):
        need("t", cs["cv"], cs["ci"], ce[c])
        for k in range(4 * c, 4 * c + 4):
            inst = t.matmul(T.ps7[:, 0:F], lhs, T.P[:, F * k:F * k + F], k == 0 and not kinds, k == N - 1)
        if c == 2:
            done(inst, last)

    masks(0)
    behind(0)
    step(0)
    masks(1)
    behind(1)
    step(1)
    scan(0)
    lower(0)
    masks(2)
    behind(2)
    scan(1)
    lower(1)
    step(2)
    base(0)
    cut("s", 0)
    step(3)
    scan(2)
    lower(2)
    base(1)
    cut("v", 0)
    cut("s", 1)
    cut("v", 1)
    base(2)
    cut("v", 2)
    cut("s", 2)
    step(4)
    add(0)
    add(1)
    add(2)


def codes_of(g, T, tk, load_s, load_d, extra):
    new, done, need, finish = tk
    v = g.vector
    e = new()
    need("v", load_s)
    done(v.tensor_scalar(T.HS[:], T.S[:], 8, 4080, A.arith_shift_right, A.bitwise_and), e)
    extra()
    need("v", load_d)
    done(v.tensor_scalar(T.GD[:], T.D[:], 12, None, A.arith_shift_right), e)
    need("v", e)
    c = new()
    done(v.tensor_tensor(T.CODE[:], T.HS[:], T.GD[:], A.add), c)
    need("v", c)


def columns(g, T, tk, cs, win, starts, bank, out, ev):
    new, done, need, finish = tk
    e = new()
    need("t", win, cs["cv"])
    for i, a in enumerate(starts):
        inst = g.tensor.matmul(T[bank][:, 16 * i:16 * i + 16], T.WIN[:, a:a + 128], T.REP[:], True, True)
    done(inst, e)
    n = 16 * len(starts)
    need("v", e, cs["cm"])
    done(g.vector.tensor_tensor(out, T[bank][:, 0:n], T.MK[:, 0:n], A.mult), ev)


def addr_of(core, topo, d):
    rid, pid = topo.addr(d, core)
    return DstId(rid=rid, pnc=pid)


def send_lists(g, core, T, topo, srcs, dests, eng, sem):
    h = len(eng) // 2
    trs = []
    for k in range(2):
        trs.append(RemoteDMATransfer(dst_ids=[addr_of(core, topo, d[0]) for d in dests], dma_engine_mask=together(eng[h * k:h * k + h]),
                                     remote_sem=sem, srcs=[srcs[k]], dsts=[d[1 + k] for d in dests]))
    g.remote_dma_fused(trs, local_sem=T.sem.ls)
    return len(eng)


def send_block(g, core, T, topo, dest, out, in_, sem, eng=None):
    eng = eng or shared_engines(topo, core, [dest])
    rid, pid = topo.addr(dest, core)
    g.remote_dma(out, in_, sem, T.sem.ls, pid, rid, together(eng))
    return len(eng)


def landing(T, h):
    return T.W[:, R + CAPP * h:R + CAPP * h + CAPP]


def relay_list(g, core, T, topo, buf, r):
    peer = layout(T, topo, r)[0]
    off = leaving_engines(topo, core)
    k = slot_of(T, topo, peer)
    ds = [other_helper_of(T.cores[t], topo) for t in layout(T, topo, peer)[1]]
    g.wait_ge(T.sem.lp, len(off) // 2)
    tr = RemoteDMATransfer(dst_ids=[addr_of(core, topo, d) for d in ds], dma_engine_mask=together(off), remote_sem=T.sem.la,
                           srcs=[buf[k]], dsts=[buf[k] for d in ds])
    g.remote_dma_fused([tr], local_sem=T.sem.ls)
    return len(off)


def relay_block(g, core, T, topo, r, i):
    peer = layout(T, topo, r)[0]
    t = layout(T, topo, peer)[1][i]
    g.wait_ge(T.sem["di%d" % i], len(leaving_engines(topo, core)))
    return send_block(g, core, T, topo, T.cores[t], landing(T, peer), T.DG[:, CAPP * i:CAPP * i + CAPP], T.sem.da)


def load_lists(g, T, tk, waits):
    new, done, need, finish = tk
    ls, ld = new(), new()
    for sem, n in waits:
        g.sync.wait_ge(sem, n)
        g.scalar.wait_ge(sem, n)
    done(g.sync.dma_start(T.S[:], T.Ls[:]), ls, 16)
    done(g.scalar.dma_start(T.D[:], T.Ld[:]), ld, 16)
    return ls, ld


def forwarded(far):
    return far[2]


def shares(r, diag, far, mate, same):
    return [diag[2], forwarded(far), far[1]] + same + [mate[2], r], [diag[0], diag[1], far[0]] + mate[:2]


def gathered(T, r, d, i, a, b):
    if d == r:
        return T.W[:, R + CAPP * r + a:R + CAPP * r + b]
    return T.G[:, CAPP * i + a:CAPP * i + b]


def source(g, core, T, topo, r, is_rank):
    tk = tools(g, T)
    new, done, need, finish = tk
    v, s, t = g.vector, g.scalar, g.tensor
    peer, diag, far, mate, same = layout(T, topo, r)
    rank = T.cores[r]
    sec = second_of(rank, topo)
    pc = T.cores[peer]
    down = downwards(T, topo, r, is_rank)
    off = leaving_engines(topo, core)
    ne = len(off)
    h = ne // 2
    left = 0
    tabs = [new(), new()]

    def load_table(j):
        a = R // 2 * j
        done(g.sync.dma_start(T.W[:, a:a + R // 2], T.tab[:, a:a + R // 2]), tabs[j], 16)

    def copy_table(j):
        a = R // 2 * j
        need("g", tabs[j])
        return send_block(g, core, T, topo, sec, T.W[:, a:a + R // 2], T.W[:, a:a + R // 2], T.sem.tb)

    if is_rank:
        k = slot_of(T, topo, r)
        pr = new()
        done(g.sync.dma_start(T.Ls[k], T.src[:]), pr, 16)
        done(s.dma_start(T.Ld[k], T.dst[:]), pr, 16)
        cs = constants(g, T, tk, True, down)
        need("y", pr)
        load_table(0)
        need("g", pr)
        srcs = [T.Ls[k], T.Ld[k]]
        ds = [second_of(pc, topo), other_helper_of(pc, topo), helper_of(core, topo)]
        left += send_lists(g, core, T, topo, srcs, [(pc, T.Ps[0], T.Pd[0])] + [(c, T.Ls[k], T.Ld[k]) for c in ds], off[:h], T.sem.lp)
        rest = [d for d in far if d != peer]
        ds = [second_of(T.cores[d], topo) for d in rest] + [T.cores[d] for d in mate + same] + [other_helper_of(T.cores[d], topo) for d in rest]
        left += send_lists(g, core, T, topo, srcs, [(c, T.Ls[k], T.Ld[k]) for c in ds], off[h:], T.sem.la)
        g.wait_ge(T.sem.lp, h)
        p = slot_of(T, topo, peer)
        ds = [second_of(T.cores[d], topo) for d in layout(T, topo, peer)[1]]
        left += send_lists(g, core, T, topo, [T.Ps[0], T.Pd[0]], [(c, T.Ls[p], T.Ld[p]) for c in ds], off[:h], T.sem.la)
        cg = cs["late"]()
        need("s", pr)
        load_s, load_d = load_lists(g, T, tk, [(T.sem.la, h * (NL - 1))])
        load_table(1)
        left += copy_table(0)
        left += copy_table(1)
    else:
        cs = constants(g, T, tk, True, down)
        cg = cs["late"]()
        left += relay_list(g, core, T, topo, T.Ls, r)
        load_s, load_d = load_lists(g, T, tk, [(T.sem.lp, h), (T.sem.la, h * (NL - 1))])

    sl, hi, lo, nm, nk = new(), new(), new(), new(), new()

    def take_sl():
        done(v.tensor_scalar(T.SL[:], T.S[:], float(-R * r), None, A.add), sl)
        need("s", sl)
        done(s.activation(T.HI[:], T.SL[:], COPY), hi)

    codes_of(g, T, tk, load_s, load_d, take_sl)
    vv, ee, x = new(), new(), new()
    bank = [T.ps3[:, 0:F], T.ps6[:, 0:F]]

    def kinds(c, me):
        need("t", cs["si"], me)
        for d in range(max(1, 4 * c), 4 * c + 4):
            a = CW * c + KW * (d % 4) + 1
            t.matmul(T.ps7[:, 0:F], T.DI[:, 128 * d:128 * d + 128], T.MA[:, a:a + F], d == 1, False)

    def step(c):
        if c == 0:
            need("v", sl, hi)
            done(v.tensor_tensor(T.LO[:], T.SL[:], T.HI[:], A.subtract), lo)
            need("t", cs["cv"], hi, lo)
            for j in range(2):
                done(t.matmul(bank[j], T.PRM[:, 256 * j:256 * j + 128], T.HI[:], True, False), ee)
                done(t.matmul(bank[j], T.PRM[:, 256 * j + 128:256 * j + 256], T.LO[:], False, True), ee)
        if c == 1:
            need("s", cs["cv"], ee)
            spread(("s", s), T, tk, vv, range(0, 6, 2), bank)
        if c == 2:
            done(v.tensor_scalar(T.NM[:], T.HS[:], float(16 * r), None, A.not_equal), nm)
            spread(("s", s), T, tk, vv, range(6, 12, 2), bank)
        if c == 3:
            need("v", nm, cg)
            done(v.tensor_tensor(T.NK[:], T.NM[:], T.K16[:], A.mult), nk)
        if c == 4:
            spread(("s", s), T, tk, vv, [12, 14] + list(range(1, 16, 2)), bank)
            need("t", nm, nk)
            t.matmul(T.ps7[:, 0:F], T.DQ[:], T.NM[:], False, False)
            t.matmul(T.ps7[:, 0:F], T.IDN[:], T.NK[:], False, False)

    numbers(g, T, tk, cs, [16 * r + d for d in range(N)], T.NID[:] if down else T.IDN[:], (3, 3, 3), step, x, kinds)
    o = new()
    need("v", x)
    done(v.tensor_scalar(T.O[:], T.ps7[:, 0:F], float(TR + 255 if down else TR), None, A.add), o)
    need("v", o, vv)
    win = new()
    done(v.tensor_copy(T.WIN[:, 0:TR + LAND].indirect(T.O[:]), T.V[:]), win)
    ours, hers = shares(r, diag, far, mate, same)
    if not is_rank:
        ours, hers = hers, ours
    rx, ro, ge, go = [[new(), new()] for _ in range(4)]

    def halfway(ts, out, banks, ev):
        for c, (a, b) in enumerate(PARTS):
            starts = [TR + CAPP * d + u for d in ts[a:b] for u in (0, 128)]
            columns(g, T, tk, cs, win, starts, banks[c], out[:, BC * a:BC * min(b, len(ts))], ev[c])

    halfway(hers, T.RX, ("ps4", "ps5"), rx)
    halfway(ours, T.RO, ("ps1", "ps2"), ro)
    for c, (a, b) in enumerate(PARTS):
        need("g", rx[c])
        b = min(b, len(hers))
        left += send_block(g, core, T, topo, sec if is_rank else rank, T.RI[:, BC * a:BC * b], T.RX[:, BC * a:BC * b], T.sem["xs%d" % c], off)
    if is_rank:
        need("v", *tabs)
        need("s", *tabs)
    else:
        for q in (v, s):
            q.wait_ge(T.sem.tb, 2 * len(shared_engines(topo, rank, [core])))
    for c, (a, b) in enumerate(PARTS):
        b = min(b, len(ours))
        out = T[("ps0", "ps6")[c]][:, 0:16 * (b - a)]
        need("t", ro[c], cs["cm"])
        t.matmul(out, T.L16[:], T.RO[:, BC * a:BC * b:2], True, False)
        t.matmul(out, T.L16[:], T.RO[:, BC * a + 1:BC * b:2], False, False)
        t.wait_ge(T.sem["xs%d" % c], ne)
        t.matmul(out, T.L16[:], T.RI[:, BC * a:BC * b:2], False, False)
        done(t.matmul(out, T.L16[:], T.RI[:, BC * a + 1:BC * b:2], False, True), ge[c])
        need("v", ge[c])
        done(v.tensor_copy(T.GO[:, 16 * a:16 * b], out), go[c])
        need("v", go[c])
        need("s", go[c])
        for i in range(a, b):
            d = ours[i]
            e = new()
            cols = [("vs"[(i - a) % 2], 0, CAPP)]
            if i == b - 1 and (b - a) % 2:
                cols = [("v", 0, CAPP // 2), ("s", CAPP // 2, CAPP)]
            for q, x0, x1 in cols:
                src = T.W[:, 0:R].indirect(T.GO[:, 16 * i + x0 // 16:16 * i + x1 // 16])
                if q == "v":
                    done(v.tensor_copy(gathered(T, r, d, i, x0, x1), src), e)
                else:
                    done(s.activation(gathered(T, r, d, i, x0, x1), src, COPY), e)
            if d == r:
                own = e
                continue
            need("g", e)
            blk = gathered(T, r, d, i, 0, CAPP)
            if d in diag:
                j = diag.index(d)
                to = diag_sender(j, helper_of(pc, topo), other_helper_of(pc, topo))
                left += send_block(g, core, T, topo, to, T.DG[:, CAPP * j:CAPP * j + CAPP], blk, T.sem["di%d" % j])
            elif d == forwarded(far):
                to = helper_of(rank, topo)
                inside = [b_ for b_ in shared_engines(topo, core, [to]) if b_ not in off]
                left += send_block(g, core, T, topo, to, T.FW[:], blk, T.sem.fw, inside)
            else:
                left += send_block(g, core, T, topo, T.cores[d], landing(T, r), blk, T.sem.da)
    if is_rank:
        cg2, tc, inv, ej, y0 = new(), new(), new(), new(), new()
        done(g.iota(T.TC[:], [[16, R // 16]], 0, 0, allow_small_or_imprecise_dtypes=True), cg2)
        need("v", cg2)
        done(v.tensor_scalar(T.TC[:], T.TC[:], T.QF[:, 0:1], None, A.add), tc)
        t.wait_ge(T.sem.iv, 2 * ne)
        out = T.ps7[:, 0:R // 16]
        t.matmul(out, T.L16[:], T.RA[:, 0:512:2], True, False)
        t.matmul(out, T.L16[:], T.RA[:, 1:512:2], False, False)
        t.matmul(out, T.L16[:], T.RB[:, 0:512:2], False, False)
        done(t.matmul(out, T.L16[:], T.RB[:, 1:512:2], False, True), y0)
        need("v", y0, tc)
        done(v.tensor_tensor(T.EE[:], T.TC[:], out, A.max), ej)
        need("v", ej)
        done(v.tensor_copy(T.INV[:], T.EE[:]), inv)
        for q in (v, s):
            q.wait_ge(T.sem.da, ne * (N - 1))
        need("v", inv, own)
        need("s", inv, own)
        at = 0
        yo = new()
        for j, w in enumerate((640, 640, 768, 768, 640, 640)):
            src = T.W[:].indirect(T.INV[:, at // 16:(at + w) // 16])
            e = new()
            if j % 2 == 0:
                done(v.tensor_copy(T.Y[:, at:at + w], src), e)
            else:
                done(s.activation(T.Y[:, at:at + w], src, COPY), e)
            need("y", e)
            done(g.sync.dma_start(T.y[:, at:at + w], T.Y[:, at:at + w]), yo, 16)
            at += w
        need("y", yo)
    g.wait_ge(T.sem.ls, left)
    finish()


def helper(g, core, T, topo, r, own):
    tk = tools(g, T)
    new, done, need, finish = tk
    v, s, t = g.vector, g.scalar, g.tensor
    peer, diag, far, mate, same = layout(T, topo, r)
    down = downwards(T, topo, r, own)
    off = leaving_engines(topo, core)
    ne = len(off)
    left = 0
    cs = constants(g, T, tk, False, down)
    cg = cs["late"]()
    td = [new(), new()]
    mine, place = T.U[:, 3 * F:4 * F], T.U[:, 4 * F:5 * F]
    need("v", cg, cs["q"])
    done(v.tensor_scalar(place, T.K16[:], T.QF[:, 0:1], None, A.add), td[0])
    need("v", td[0])
    done(v.tensor_scalar(T.U[:, 5 * F:6 * F], place, float(R * r), None, A.add), td[1])
    if own:
        g.wait_ge(T.sem.lp, ne // 2)
        k = slot_of(T, topo, r)
        ds = [(helper_of(T.cores[d], topo), T.Ls[k], T.Ld[k]) for d in mate + same]
        left += send_lists(g, core, T, topo, [T.Ls[k], T.Ld[k]], ds, off, T.sem.la)
        waits = [(T.sem.lp, ne // 2), (T.sem.la, ne * (NL - 1))]
    else:
        left += relay_list(g, core, T, topo, T.Ld, r)
        waits = [(T.sem.lp, ne // 2), (T.sem.la, ne // 2 * 2 + ne * 6)]
    load_s, load_d = load_lists(g, T, tk, waits)
    codes_of(g, T, tk, load_s, load_d, lambda: None)
    a, hi, b, c, o, oo = new(), new(), new(), new(), new(), new()
    x, lo, ee, vv = new(), new(), [new(), new()], new()
    bank = [T.ps3[:, 0:F], T.ps6[:, 0:F]]

    def step(ch):
        if ch == 2:
            done(v.tensor_scalar(T.HI[:], T.HS[:], float(CAPP // 16), float(R), A.mult, A.add), hi)
            need("t", cs["cv"], hi)
            for j in range(2):
                t.matmul(bank[j], T.PRM[:, 256 * j:256 * j + 128], T.HI[:], True, False)
        if ch == 3:
            done(v.tensor_scalar(mine, T.GD[:], float(r), None, A.is_equal), a)
            need("v", td[1])
            done(v.tensor_tensor(T.U[:, 0:F], T.D[:], T.U[:, 5 * F:6 * F], A.subtract), b)

    numbers(g, T, tk, cs, [16 * d + r for d in range(N)], T.IDN[:], (1, 2, 2), step, x, None)
    need("s", x)
    if down:
        done(s.activation(T.LO[:], T.ps7[:, 0:F], RELU, bias=255.0, scale=-1.0), lo)
    else:
        done(s.activation(T.LO[:], T.ps7[:, 0:F], COPY), lo)
    need("t", lo)
    for j in range(2):
        done(t.matmul(bank[j], T.PRM[:, 256 * j + 128:256 * j + 256], T.LO[:], False, True), ee[j])
    need("v", a, b)
    done(v.tensor_tensor(T.U[:, F:2 * F], T.U[:, 0:F], mine, A.mult), c)
    need("v", c)
    done(v.tensor_tensor(T.U[:, 2 * F:3 * F], T.U[:, F:2 * F], place, A.add), o)
    need("v", o)
    done(v.tensor_copy(T.O[:], T.U[:, 2 * F:3 * F]), oo)
    need("s", cs["cv"], ee[0])
    spread(("s", s), T, tk, vv, range(0, 16, 2), bank)
    need("v", ee[1])
    spread(("v", v), T, tk, vv, range(1, 16, 2), bank)
    need("v", oo, vv)
    win = new()
    done(v.tensor_copy(T.WIN[:, 0:R + TR].indirect(T.O[:]), T.V[:]), win)
    rh = new()
    for k in range(4):
        starts = range(1024 * k, 1024 * k + 1024, 128)
        columns(g, T, tk, cs, win, starts, ("ps4", "ps5", "ps0", "ps1")[k], T.RH[:, 128 * k:128 * k + 128], rh)
    need("g", rh)
    left += send_block(g, core, T, topo, T.cores[r], T.RA[:] if own else T.RB[:], T.RH[:], T.sem.iv, off)
    for i in (0, 2, 1):
        if diag_sender(i, True, False) == own:
            left += relay_block(g, core, T, topo, r, i)
    if own:
        g.wait_ge(T.sem.fw, ne)
        left += send_block(g, core, T, topo, T.cores[forwarded(far)], landing(T, r), T.FW[:], T.sem.da)
    g.wait_ge(T.sem.ls, left)
    finish()


def rank_program(g, core, T, topo):
    for r in range(N):
        c = T.cores[r]
        if core == c:
            source(g, core, T, topo, r, True)
            return
        if core == second_of(c, topo):
            source(g, core, T, topo, r, False)
            return
        if core == helper_of(c, topo):
            helper(g, core, T, topo, r, True)
            return
        if core == other_helper_of(c, topo):
            helper(g, core, T, topo, r, False)
            return
